import numpy as np
import ml_dtypes


def mxq(x, axis, fmt="e4m3"):
    dtype, down = {"e4m3": (ml_dtypes.float8_e4m3fn, 7), "e5m2": (ml_dtypes.float8_e5m2, 14)}[fmt]
    v = np.moveaxis(np.asarray(x, np.float32).astype(ml_dtypes.bfloat16).astype(np.float64), axis, -1)
    blocks = v.reshape(v.shape[:-1] + (-1, 32))
    amax = np.abs(blocks).max(-1, keepdims=True)
    byte = np.maximum(np.where(amax > 0, np.frexp(amax)[1] - 1 + 127, 0) - down, 1)
    scale = np.exp2(byte - 127.0)
    codes = (blocks / scale).astype(np.float32).astype(dtype).astype(np.float64)
    return np.moveaxis((codes * scale).reshape(v.shape), -1, axis)


WIDE = False


def mx_kscale(k):
    if not WIDE:
        return np.ones(k)
    levels = np.array([10, -10, 5, -5, 0])
    if k % 512:
        return np.exp2(np.random.permutation(np.resize(levels, k // 32))).repeat(32)
    a = np.empty((k // 512, 16))
    for p in range(k // 512):
        a[p, :8] = np.random.permutation(np.resize(levels, 8))
        for g in range(8):
            far = levels[np.abs(levels - a[p, g]) >= 10]
            a[p, g + 8] = far[np.random.randint(len(far))]
    return np.exp2(a.ravel()).repeat(32)


def f64(x):
    return np.asarray(x).astype(np.float64)


E2M1 = np.array([0.0, 0.5, 1.0, 1.5, 2.0, 3.0, 4.0, 6.0, -0.0, -0.5, -1.0, -1.5, -2.0, -3.0, -4.0, -6.0])


def pack_weight(w, fmt):
    k, n = w.shape
    w = f64(np.asarray(w, np.float32).astype(ml_dtypes.bfloat16)).reshape(k // 32, 32, n)
    amax = np.abs(w).max(1)
    if fmt == "e4m3":
        byte = np.frexp(amax)[1] - 1 + 127 - 7
    else:
        mant, ex = np.frexp(amax / 6.0)
        byte = np.where(mant > 0.5, ex, ex - 1) + 127
    byte = np.clip(np.where(amax > 0, byte, 1), 1, 254)
    scaled = (w * np.exp2(127.0 - byte)[:, None, :]).reshape(k, n).astype(np.float32)
    by_word = np.ascontiguousarray(scaled.reshape(k // 512, 128, 4, n).transpose(0, 1, 3, 2))
    if fmt == "e4m3":
        words = by_word.astype(ml_dtypes.float8_e4m3fn).view(np.uint8)
    else:
        c = by_word.astype(ml_dtypes.float4_e2m1fn).view(np.uint8) & 0xF
        words = (c[..., 0::2] | (c[..., 1::2] << 4)).reshape(k // 512, 128, 2 * n)
    return np.ascontiguousarray(words), np.ascontiguousarray(byte.astype(np.uint8).reshape(k // 512, 16, n))


def unpack_weight(words, scales, fmt):
    g, _, n = scales.shape
    words = np.ascontiguousarray(words).reshape(g, 128, n, -1)
    if fmt == "e4m3":
        vals = words.view(ml_dtypes.float8_e4m3fn).astype(np.float64)
    else:
        nib = np.empty((g, 128, n, 4), np.uint8)
        nib[..., 0::2] = words & 0xF
        nib[..., 1::2] = words >> 4
        vals = E2M1[nib]
    vals = vals * np.repeat(np.exp2(scales.astype(np.float64) - 127.0), 8, axis=1)[..., None]
    return vals.transpose(0, 1, 3, 2).reshape(g * 512, n)


def planes(y):
    n, m = y.shape
    v = y.astype(np.float32).astype(ml_dtypes.bfloat16).astype(np.float64).reshape(n // 32, 32, m)
    top = np.abs(v).max(1)
    byte = np.clip(np.where(top > 0, np.frexp(top)[1] - 1 + 127 - 7, 1), 1, 254)
    codes = (v * np.exp2(127.0 - byte)[:, None, :]).reshape(n, m).astype(np.float32).astype(ml_dtypes.float8_e4m3fn).view(np.uint8)
    words = codes.reshape(n // 512, 128, 4, m).transpose(0, 1, 3, 2)
    return np.ascontiguousarray(words), np.ascontiguousarray(byte.astype(np.uint8).reshape(n // 512, 16, m))


def silu(v):
    return v / (1.0 + np.exp(-np.maximum(v, -700.0)))


O, K, M, T = 512, 1536, 1024, 1024


def setup_inputs():
    n = np.random.standard_normal
    s = mx_kscale(K)[:, None]
    x = n((K, T)); x[:O] *= 6.0
    w = n((K, M)) / np.sqrt(K) / s; w[:O] /= 2.0
    p_x4 = pack_weight(x[O:] * s[O:], "e2m1")
    p_w4 = pack_weight(w[O:], "e2m1")
    return {
        "x8": (x[:O] * s[:O]).astype(np.float32),
        "w8": (w[:O]).astype(np.float32),
        "x4_words": p_x4[0],
        "x4_scales": p_x4[1],
        "w4_words": p_w4[0],
        "w4_scales": p_w4[1],
        "b": (0.3 * n(1024)).astype(np.float32),
    }


def reference(x8, w8, x4_words, x4_scales, w4_words, w4_scales, b):
    x8_ = mxq(f64(x8), 0, "e4m3")
    w8_ = mxq(f64(w8), 0, "e4m3")
    x4_ = unpack_weight(x4_words, x4_scales, "e2m1")
    w4_ = unpack_weight(w4_words, w4_scales, "e2m1")
    y = x8_.T @ w8_ + x4_.T @ w4_
    out_0 = silu(y + f64(b)[None, :])
    return (out_0,) + planes(out_0)

@@ -1,0 +1,416 @@
+from contextlib import ExitStack
+
+import concourse.mybir as mybir
+from concourse.masks import make_identity
+
+O, K4, M, T = 512, 1024, 1024, 1024
+FLOPS = 2 * (O + K4) * M * T
+
+F32 = mybir.dt.float32
+BF16 = mybir.dt.bfloat16
+I32 = mybir.dt.int32
+U32 = mybir.dt.uint32
+U8 = mybir.dt.uint8
+FP8X4 = mybir.dt.float8_e4m3fn_x4
+FP4X4 = mybir.dt.float4_e2m1fn_x4
+SILU = mybir.ActivationFunctionType.Silu
+ADD = mybir.AluOpType.add
+MULT = mybir.AluOpType.mult
+
+P = 128
+PACK = 4
+HALF = 512
+G4 = 2
+
+UNITS = [(0, 0, 256), (0, 256, 256), (1, 0, 512), (0, 512, 512), (1, 512, 512)]
+STEPS = [
+    ("setup",),
+    ("load_w8", 0, 256,),
+    ("load_x4", 1,),
+    ("load_xs", "SP",),
+    ("load_x4", 0,),
+    ("bias_tr",),
+    ("load_w4", 0,),
+    ("cast_w8", "S", 0, 256,),
+    ("load_x8", 0,),
+    ("deal_x4", 1, 0,),
+    ("load_w8", 256, 256,),
+    ("load_x8", 1,),
+    ("deal_xs", 1,),
+    ("load_ws", "S",),
+    ("bias_cp", 1,),
+    ("deal_x4", 0, 0,),
+    ("deal_xs", 0,),
+    ("load_w8", 512, 512,),
+    ("bias_cp", 0,),
+    ("deal_x4", 0, 1,),
+    ("quant_w8", 0, 256,),
+    ("deal_x4", 1, 1,),
+    ("mm4", 0, 2,),
+    ("cast_x8", "S", 0, 0,),
+    ("cast_x8", "V", 0, 1,),
+    ("load_w4", 1,),
+    ("mm4", 1, 2,),
+    ("mm4", 0, 3,),
+    ("quant_x8", 0, 1,),
+    ("mm4", 0, 0,),
+    ("cast_w8", "V", 256, 256,),
+    ("mm4", 0, 1,),
+    ("mm8", 0, 3,),
+    ("quant_x8", 0, 0,),
+    ("mm4", 1, 3,),
+    ("add", 0, 3,),
+    ("mm8", 0, 2,),
+    ("mm8", 0, 1,),
+    ("quant_w8", 256, 256,),
+    ("mm8", 0, 0,),
+    ("add", 0, 2,),
+    ("mm4", 1, 1,),
+    ("mm8", 1, 3,),
+    ("add", 0, 1,),
+    ("mm4", 1, 0,),
+    ("silu", 0, 2, 4,),
+    ("mm8", 1, 0,),
+    ("mm8", 1, 2,),
+    ("add", 0, 0,),
+    ("add", 1, 3,),
+    ("cast_x8", "S", 1, 0,),
+    ("cast_x8", "V", 1, 1,),
+    ("mm4", 2, 1,),
+    ("mm8", 1, 1,),
+    ("add", 1, 2,),
+    ("mm4", 2, 2,),
+    ("quant_x8", 1, 1,),
+    ("silu", 0, 0, 2,),
+    ("add", 1, 1,),
+    ("mm4", 2, 3,),
+    ("add", 1, 0,),
+    ("mm8", 2, 2,),
+    ("silu", 1, 2, 4,),
+    ("quant_x8", 1, 0,),
+    ("mm8", 2, 3,),
+    ("store_res", 0, 0, 4,),
+    ("add", 2, 2,),
+    ("silu", 1, 0, 2,),
+    ("mm4", 2, 0,),
+    ("cast_w8", "V", 512, 256,),
+    ("mm8", 2, 0,),
+    ("add", 2, 0,),
+    ("cast_w8", "S", 768, 256,),
+    ("mm8", 2, 1,),
+    ("mm4", 3, 2,),
+    ("quant_w8", 512, 256,),
+    ("cast_res", "S", 1, 0, 256,),
+    ("store_res", 1, 0, 4,),
+    ("add", 2, 1,),
+    ("mm4", 3, 0,),
+    ("quant_w8", 768, 256,),
+    ("mm4", 3, 1,),
+    ("add", 2, 3,),
+    ("mm4", 4, 0,),
+    ("silu", 2, 0, 1,),
+    ("mm8", 3, 0,),
+    ("cast_res", "V", 0, 0, 256,),
+    ("mm8", 4, 0,),
+    ("mm8", 3, 2,),
+    ("silu", 2, 1, 2,),
+    ("mm8", 3, 1,),
+    ("store_res", 2, 0, 2,),
+    ("add", 3, 0,),
+    ("silu", 2, 2, 3,),
+    ("silu", 2, 3, 4,),
+    ("mm4", 4, 3,),
+    ("mm8", 4, 3,),
+    ("mm4", 3, 3,),
+    ("add", 3, 1,),
+    ("add", 3, 2,),
+    ("silu", 3, 0, 1,),
+    ("store_res", 2, 2, 4,),
+    ("silu", 3, 1, 2,),
+    ("quant_res", 0, 0, 256,),
+    ("mm8", 3, 3,),
+    ("mm4", 4, 1,),
+    ("add", 4, 0,),
+    ("cast_res", "S", 2, 128, 256,),
+    ("quant_res", 1, 0, 256,),
+    ("store_res", 3, 0, 2,),
+    ("mm4", 4, 2,),
+    ("add", 3, 3,),
+    ("mm8", 4, 2,),
+    ("silu", 3, 2, 3,),
+    ("mm8", 4, 1,),
+    ("store_codes", 0, 0, 512,),
+    ("add", 4, 3,),
+    ("silu", 4, 0, 1,),
+    ("silu", 3, 3, 4,),
+    ("add", 4, 2,),
+    ("silu", 4, 3, 4,),
+    ("add", 4, 1,),
+    ("store_res", 3, 2, 4,),
+    ("silu", 4, 2, 3,),
+    ("cast_res", "V", 3, 0, 128,),
+    ("silu", 4, 1, 2,),
+    ("cast_res", "V", 3, 256, 384,),
+    ("store_res", 4, 2, 4,),
+    ("cast_res", "V", 2, 384, 512,),
+    ("cast_res", "V", 3, 128, 256,),
+    ("cast_res", "S", 3, 384, 512,),
+    ("cast_res", "V", 2, 0, 128,),
+    ("quant_res", 3, 0, 256,),
+    ("cast_res", "S", 2, 256, 384,),
+    ("cast_res", "V", 4, 256, 384,),
+    ("quant_res", 2, 0, 256,),
+    ("cast_res", "S", 4, 128, 256,),
+    ("quant_res", 3, 256, 512,),
+    ("cast_res", "V", 4, 384, 512,),
+    ("store_res", 4, 0, 2,),
+    ("cast_res", "S", 4, 0, 128,),
+    ("store_codes", 0, 512, 512,),
+    ("quant_res", 2, 256, 512,),
+    ("store_codes", 1, 0, 512,),
+    ("quant_res", 4, 256, 512,),
+    ("quant_res", 4, 0, 256,),
+    ("store_scales", "SP", 3,),
+    ("store_scales", "S", 2,),
+    ("store_scales", "S", 0,),
+    ("store_scales", "SP", 1,),
+    ("store_codes", 1, 512, 512,),
+]
+
+
+def tile_mix_atom_tm_pl_silu_kernel(
+    tc, x8, w8, x4_words, x4_scales, w4_words, w4_scales, b, out_0, out_1, out_2
+):
+    nc = tc.nc
+    with ExitStack() as ctx:
+        sb = ctx.enter_context(tc.tile_pool(name="sb", bufs=1))
+        ps = ctx.enter_context(tc.psum_pool(name="ps", bufs=1))
+        ctx.enter_context(tc.manual_schedule())
+
+        def tile(name, shape, dtype):
+            return sb.tile(shape, dtype, name=name, align_bytes=64)
+
+        banks = [ps.tile([P, 512], F32, name="bank%d" % i) for i in range(8)]
+
+        x4_raw = [tile("x4_raw%d" % a, [P, G4, 2 * HALF], U8) for a in range(2)]
+        xs_raw = tile("xs_raw", [P, G4, T], U8)
+        x4_dealt = [tile("x4_dealt%d" % a, [P, G4, PACK, 2 * P], U8) for a in range(2)]
+        xs_dealt = [tile("xs_dealt%d" % a, [P, G4, PACK, P], U8) for a in range(2)]
+        w4 = [tile("w4_%d" % h, [P, G4, 2 * HALF], U8) for h in range(2)]
+        ws = tile("ws", [P, G4, M], U8)
+        x8_raw = [tile("x8_raw%d" % a, [P, PACK, HALF], F32) for a in range(2)]
+        x8_bf = [[tile("x8_bf%d_%d" % (a, s), [P, 2, P, PACK], BF16) for s in range(2)] for a in range(2)]
+        x8_codes = [tile("x8_codes%d" % a, [P, PACK * P], U32) for a in range(2)]
+        x8_scales = [tile("x8_scales%d" % a, [P, PACK * P], U8) for a in range(2)]
+        w8_codes = tile("w8_codes", [P, M], U32)
+        w8_scales = tile("w8_scales", [P, M], U8)
+        w8_raw = {}
+        w8_bf = tile("w8_bf", [P, M, PACK], BF16)
+        b_rows = tile("b_rows", [P, 8], F32)
+        ident = tile("ident", [P, P], F32)
+        bias = tile("bias", [P, M], F32)
+        warm = tile("warm", [P, 8], F32)
+        res = [tile("res%d" % u, [P, PACK, UNITS[u][2]], F32) for u in range(len(UNITS))]
+        pre = [tile("pre%d" % u, [P, PACK, UNITS[u][2]], F32) for u in range(len(UNITS))]
+        res_bf = [tile("res_bf%d" % u, [P, UNITS[u][2], PACK], BF16) for u in range(len(UNITS))]
+        out_codes = tile("out_codes", [P, 2, M], U32)
+        out_scales = tile("out_scales", [P, 2, M], U8)
+
+        def interleave(eng, dst, src):
+            cast(eng, dst.rearrange("p (c i) j -> p c j i", i=4), src.rearrange("p j (c i) -> p c j i", i=4))
+
+        def load_scales(queue, plane, scales):
+            for q in range(4):
+                queue.dma_start(
+                    out=plane[32 * q : 32 * q + 4, :, :].bitcast(I32),
+                    in_=scales[:, 4 * q : 4 * q + 4, :].rearrange("g r n -> r g n").bitcast(I32),
+                )
+
+        def load_x4(a):
+            nc.sync.dma_start(
+                out=x4_raw[a][:].bitcast(I32),
+                in_=x4_words[:, :, 2 * HALF * a : 2 * HALF * (a + 1)].rearrange("g p c -> p g c").bitcast(I32),
+            )
+
+        def load_w4(h):
+            nc.sync.dma_start(
+                out=w4[h][:].bitcast(I32),
+                in_=w4_words[:, :, 2 * HALF * h : 2 * HALF * (h + 1)].rearrange("g p c -> p g c").bitcast(I32),
+            )
+
+        def load_w8(n0, width):
+            raw = tile("w8_raw%d" % n0, [P, PACK, width], F32)
+            w8_raw[n0] = raw
+            nc.sync.dma_start(out=raw[:], in_=w8[:, n0 : n0 + width].rearrange("(p j) n -> p j n", j=PACK))
+
+        def load_x8(a):
+            nc.sync.dma_start(
+                out=x8_raw[a][:], in_=x8[:, HALF * a : HALF * (a + 1)].rearrange("(p j) t -> p j t", j=PACK)
+            )
+
+        def bias_tr():
+            for e in range(8):
+                nc.tensor.transpose(
+                    banks[6 + e // 4][:, P * (e % 4) : P * (e % 4 + 1)],
+                    b_rows[:, e : e + 1].to_broadcast([P, P]),
+                    ident[:],
+                )
+
+        def bias_cp(half):
+            nc.scalar.copy(
+                out=bias[:].rearrange("p (m e) -> p m e", e=8)[:, :, 4 * half : 4 * half + 4],
+                in_=banks[6 + half][:].rearrange("p (e m) -> p m e", e=4),
+            )
+
+        def deal_x4(a, g):
+            nc.vector.tensor_copy(
+                out=x4_dealt[a][:, g].rearrange("p r (m y) -> p r m y", y=2),
+                in_=x4_raw[a][:, g, :].rearrange("p (m r y) -> p r m y", r=PACK, y=2),
+            )
+
+        def deal_xs(a):
+            nc.vector.tensor_copy(
+                out=xs_dealt[a][:],
+                in_=xs_raw[:, :, HALF * a : HALF * (a + 1)].rearrange("p g (m r) -> p g r m", r=PACK),
+            )
+
+        def cast_x8(eng, a, s):
+            cast(
+                eng,
+                x8_bf[a][s][:].rearrange("p r m j -> p m j r"),
+                x8_raw[a][:].rearrange("p j (m r) -> p m j r", r=PACK)[:, :, :, 2 * s : 2 * s + 2],
+            )
+
+        def quant_x8(a, s):
+            cols = slice(2 * P * s, 2 * P * (s + 1))
+            nc.vector.quantize_mx(
+                out=x8_codes[a][:, cols].bitcast(FP8X4),
+                scales=x8_scales[a][:, cols],
+                in_=x8_bf[a][s][:].rearrange("p r m j -> p (r m j)"),
+            )
+
+        def cast_w8(eng, n0, width):
+            first = max(c for c in w8_raw if c <= n0)
+            interleave(eng, w8_bf[:, n0 : n0 + width, :], w8_raw[first][:, :, n0 - first : n0 - first + width])
+
+        def quant_w8(n0, width):
+            nc.vector.quantize_mx(
+                out=w8_codes[:, n0 : n0 + width].bitcast(FP8X4),
+                scales=w8_scales[:, n0 : n0 + width],
+                in_=w8_bf[:, n0 : n0 + width, :].rearrange("p c j -> p (c j)"),
+            )
+
+        def bank_of(u, r):
+            return banks[4 * (u % 2) + r][:, 0 : UNITS[u][2]]
+
+        def mm4(u, r):
+            a, n0, width = UNITS[u]
+            h, c0 = divmod(n0, HALF)
+            for g in range(G4):
+                nc.tensor.matmul_mx(
+                    out=bank_of(u, r),
+                    lhsT=x4_dealt[a][:, g, r, :].bitcast(FP4X4),
+                    lhsT_scale=xs_dealt[a][:, g, r, :],
+                    rhs=w4[h][:, g, 2 * c0 : 2 * (c0 + width)].bitcast(FP4X4),
+                    rhs_scale=ws[:, g, n0 : n0 + width],
+                    start=(g == 0),
+                    stop=False,
+                )
+
+        def mm8(u, r):
+            a, n0, width = UNITS[u]
+            nc.tensor.matmul_mx(
+                out=bank_of(u, r),
+                lhsT=x8_codes[a][:, P * r : P * (r + 1)].bitcast(FP8X4),
+                lhsT_scale=x8_scales[a][:, P * r : P * (r + 1)],
+                rhs=w8_codes[:, n0 : n0 + width].bitcast(FP8X4),
+                rhs_scale=w8_scales[:, n0 : n0 + width],
+                start=False,
+                stop=True,
+            )
+
+        def add_bias(u, r):
+            a, n0, width = UNITS[u]
+            nc.vector.tensor_tensor(out=pre[u][:, r, :], in0=bank_of(u, r), in1=bias[:, n0 : n0 + width], op=ADD)
+
+        def res_of(u):
+            return res[u][:]
+
+        def silu(u, r0, r1):
+            nc.scalar.activation(out=res_of(u)[:, r0:r1, :], in_=pre[u][:, r0:r1, :], func=SILU)
+
+        def cast_res(eng, u, c0, c1):
+            interleave(eng, res_bf[u][:, c0:c1, :], res_of(u)[:, :, c0:c1])
+
+        def quant_res(u, c0, c1):
+            a, n0, width = UNITS[u]
+            nc.vector.quantize_mx(
+                out=out_codes[:, a, n0 + c0 : n0 + c1].bitcast(FP8X4),
+                scales=out_scales[:, a, n0 + c0 : n0 + c1],
+                in_=res_bf[u][:, c0:c1, :].rearrange("p c j -> p (c j)"),
+            )
+
+        def store_res(u, r0, r1):
+            a, n0, width = UNITS[u]
+            nc.sync.dma_start(
+                out=out_0[HALF * a : HALF * (a + 1), n0 : n0 + width].rearrange("(p r) n -> p r n", r=PACK)[:, r0:r1, :],
+                in_=res[u][:, r0:r1, :],
+            )
+
+        def store_codes(a, n0, width):
+            nc.sync.dma_start(
+                out=out_1[a].rearrange("p n i -> p (n i)").bitcast(I32)[:, n0 : n0 + width],
+                in_=out_codes[:, a, n0 : n0 + width].bitcast(I32),
+            )
+
+        def store_scales(queue, q):
+            queue.dma_start(
+                out=out_2[:, 4 * q : 4 * q + 4, :].rearrange("g r n -> r g n").bitcast(I32),
+                in_=out_scales[32 * q : 32 * q + 4, :, :].bitcast(I32),
+            )
+
+        def cast(eng, dst, src):
+            if eng == "V":
+                nc.vector.tensor_copy(out=dst, in_=src)
+            elif eng == "S":
+                nc.scalar.copy(out=dst, in_=src)
+            else:
+                nc.gpsimd.tensor_scalar(out=dst, in0=src, scalar1=1.0, scalar2=0.0, op0=MULT, op1=ADD)
+
+        def setup():
+            nc.vector.memset(xs_raw[:].rearrange("p g t -> p (g t)").bitcast(I32), 0)
+            nc.vector.memset(ws[:].rearrange("p g t -> p (g t)").bitcast(I32), 0)
+            nc.vector.memset(warm[:, 0:1], 0.0)
+            nc.gpsimd.dma_start(out=b_rows[:], in_=b.rearrange("(p e) -> p e", e=8))
+            make_identity(nc, ident[:])
+            nc.scalar.activation(out=warm[:, 1:2], in_=warm[:, 0:1], func=SILU)
+
+        queues = {"SP": nc.sync, "S": nc.scalar}
+        table = {
+            "setup": setup,
+            "load_x4": load_x4,
+            "load_xs": lambda e: load_scales(queues[e], xs_raw, x4_scales),
+            "load_ws": lambda e: load_scales(queues[e], ws, w4_scales),
+            "load_w4": load_w4,
+            "load_w8": load_w8,
+            "load_x8": load_x8,
+            "bias_tr": bias_tr,
+            "bias_cp": bias_cp,
+            "deal_x4": deal_x4,
+            "deal_xs": deal_xs,
+            "cast_x8": cast_x8,
+            "quant_x8": quant_x8,
+            "cast_w8": cast_w8,
+            "quant_w8": quant_w8,
+            "mm4": mm4,
+            "mm8": mm8,
+            "add": add_bias,
+            "silu": silu,
+            "cast_res": cast_res,
+            "quant_res": quant_res,
+            "store_res": store_res,
+            "store_codes": store_codes,
+            "store_scales": lambda e, q: store_scales(queues[e], q),
+        }
+        for step in STEPS:
+            table[step[0]](*step[1:])

@@ -22,159 +22,167 @@ PACK = 4
 HALF = 512
 G4 = 2
 
-UNITS = [(0, 0, 256), (0, 256, 256), (1, 0, 512), (0, 512, 512), (1, 512, 512)]
+UNITS = [("A", 0, 0, 0, 0, 4, 256,), ("A", 0, 1, 0, 1, 4, 256,), ("A", 0, 2, 0, 2, 4, 256,), ("A", 0, 3, 0, 3, 4, 256,), ("A", 0, 0, 256, 4, 4, 256,), ("A", 0, 1, 256, 5, 4, 256,), ("A", 0, 2, 256, 6, 4, 256,), ("A", 0, 3, 256, 7, 4, 256,), ("A", 1, 0, 0, 0, 4, 512,), ("A", 1, 1, 0, 1, 4, 512,), ("A", 1, 2, 0, 2, 4, 512,), ("A", 1, 3, 0, 3, 4, 512,), ("A", 0, 0, 512, 4, 4, 512,), ("A", 0, 1, 512, 5, 4, 512,), ("A", 0, 2, 512, 6, 4, 512,), ("A", 0, 3, 512, 7, 4, 512,), ("A", 1, 0, 512, 0, 4, 512,), ("A", 1, 1, 512, 1, 4, 512,), ("A", 1, 2, 512, 2, 4, 512,), ("A", 1, 3, 512, 3, 4, 512,)]
+RES = [(0, 0, 256,), (0, 256, 256,), (1, 0, 512,), (0, 512, 512,), (1, 512, 512,)]
+DEALT = [0,1]
+BB = [5,6,7]
 STEPS = [
     ("setup",),
-    ("load_w8", 0, 256,),
-    ("load_x4", 1,),
+    ("load4", "x4", 0, 1024,),
     ("load_xs", "SP",),
-    ("load_x4", 0,),
-    ("bias_tr",),
-    ("load_w4", 0,),
-    ("cast_w8", "S", 0, 256,),
-    ("load_x8", 0,),
+    ("load4", "w4", 0, 512,),
+    ("load8", "x8", 0, 512,),
     ("deal_x4", 1, 0,),
-    ("load_w8", 256, 256,),
-    ("load_x8", 1,),
-    ("deal_xs", 1,),
-    ("load_ws", "S",),
-    ("bias_cp", 1,),
-    ("deal_x4", 0, 0,),
+    ("load_ws", "SP",),
+    ("load8", "w8", 0, 256,),
+    ("bcol_tr",),
     ("deal_xs", 0,),
-    ("load_w8", 512, 512,),
-    ("bias_cp", 0,),
-    ("deal_x4", 0, 1,),
-    ("quant_w8", 0, 256,),
+    ("load8", "w8", 256, 256,),
+    ("bcol_cp",),
     ("deal_x4", 1, 1,),
-    ("mm4", 0, 2,),
+    ("load8", "x8", 512, 512,),
+    ("bias_tr", 1,),
+    ("deal_xs", 1,),
+    ("deal_x4", 0, 0,),
+    ("bias_tr", 0,),
+    ("deal_x4", 0, 1,),
+    ("mm4", 3,),
     ("cast_x8", "S", 0, 0,),
     ("cast_x8", "V", 0, 1,),
-    ("load_w4", 1,),
-    ("mm4", 1, 2,),
-    ("mm4", 0, 3,),
+    ("load8", "w8", 512, 512,),
+    ("load4", "w4", 512, 512,),
     ("quant_x8", 0, 1,),
-    ("mm4", 0, 0,),
-    ("cast_w8", "V", 256, 256,),
-    ("mm4", 0, 1,),
-    ("mm8", 0, 3,),
+    ("bias_cp", 0,),
     ("quant_x8", 0, 0,),
-    ("mm4", 1, 3,),
-    ("add", 0, 3,),
-    ("mm8", 0, 2,),
-    ("mm8", 0, 1,),
+    ("mm4", 2,),
+    ("bias_cp", 1,),
+    ("cast_w8", "V", 0, 256,),
+    ("mm4", 0,),
+    ("mm4", 1,),
+    ("quant_w8", 0, 256,),
+    ("cast_w8", "V", 256, 256,),
+    ("mm8", 3,),
+    ("mm8", 2,),
+    ("mm8", 1,),
+    ("mm8", 0,),
+    ("add", 2,),
+    ("mm4", 6,),
     ("quant_w8", 256, 256,),
-    ("mm8", 0, 0,),
-    ("add", 0, 2,),
-    ("mm4", 1, 1,),
-    ("mm8", 1, 3,),
-    ("add", 0, 1,),
-    ("mm4", 1, 0,),
-    ("silu", 0, 2, 4,),
-    ("mm8", 1, 0,),
-    ("mm8", 1, 2,),
-    ("add", 0, 0,),
-    ("add", 1, 3,),
-    ("cast_x8", "S", 1, 0,),
+    ("mm4", 7,),
+    ("silu", 2,),
+    ("add", 3,),
+    ("mm4", 5,),
+    ("mm8", 7,),
+    ("add", 0,),
+    ("mm4", 4,),
+    ("silu", 3,),
+    ("add", 1,),
+    ("mm8", 4,),
+    ("mm8", 5,),
+    ("silu", 0,),
+    ("add", 7,),
+    ("silu", 1,),
+    ("mm4", 11,),
     ("cast_x8", "V", 1, 1,),
-    ("mm4", 2, 1,),
-    ("mm8", 1, 1,),
-    ("add", 1, 2,),
-    ("mm4", 2, 2,),
+    ("cast_x8", "S", 1, 0,),
+    ("mm8", 6,),
+    ("store_res", 0, 0, 4, 0, 256,),
+    ("mm4", 8,),
+    ("add", 4,),
     ("quant_x8", 1, 1,),
-    ("silu", 0, 0, 2,),
-    ("add", 1, 1,),
-    ("mm4", 2, 3,),
-    ("add", 1, 0,),
-    ("mm8", 2, 2,),
-    ("silu", 1, 2, 4,),
+    ("mm4", 10,),
+    ("add", 5,),
+    ("cast_res", "S", 0, 0, 128,),
+    ("mm8", 10,),
+    ("add", 6,),
+    ("mm8", 11,),
     ("quant_x8", 1, 0,),
-    ("mm8", 2, 3,),
-    ("store_res", 0, 0, 4,),
-    ("add", 2, 2,),
-    ("silu", 1, 0, 2,),
-    ("mm4", 2, 0,),
-    ("cast_w8", "V", 512, 256,),
-    ("mm8", 2, 0,),
-    ("add", 2, 0,),
-    ("cast_w8", "S", 768, 256,),
-    ("mm8", 2, 1,),
-    ("mm4", 3, 2,),
-    ("quant_w8", 512, 256,),
-    ("cast_res", "S", 1, 0, 256,),
-    ("store_res", 1, 0, 4,),
-    ("add", 2, 1,),
-    ("mm4", 3, 0,),
+    ("silu", 5,),
+    ("add", 10,),
+    ("silu", 4,),
+    ("mm4", 9,),
+    ("cast_w8", "S", 512, 256,),
+    ("mm8", 9,),
+    ("cast_w8", "V", 768, 256,),
+    ("mm8", 8,),
+    ("add", 9,),
+    ("mm4", 13,),
+    ("silu", 6,),
     ("quant_w8", 768, 256,),
-    ("mm4", 3, 1,),
-    ("add", 2, 3,),
-    ("mm4", 4, 0,),
-    ("silu", 2, 0, 1,),
-    ("mm8", 3, 0,),
-    ("cast_res", "V", 0, 0, 256,),
-    ("mm8", 4, 0,),
-    ("mm8", 3, 2,),
-    ("silu", 2, 1, 2,),
-    ("mm8", 3, 1,),
-    ("store_res", 2, 0, 2,),
-    ("add", 3, 0,),
-    ("silu", 2, 2, 3,),
-    ("silu", 2, 3, 4,),
-    ("mm4", 4, 3,),
-    ("mm8", 4, 3,),
-    ("mm4", 3, 3,),
-    ("add", 3, 1,),
-    ("add", 3, 2,),
-    ("silu", 3, 0, 1,),
-    ("store_res", 2, 2, 4,),
-    ("silu", 3, 1, 2,),
-    ("quant_res", 0, 0, 256,),
-    ("mm8", 3, 3,),
-    ("mm4", 4, 1,),
-    ("add", 4, 0,),
-    ("cast_res", "S", 2, 128, 256,),
+    ("silu", 7,),
+    ("mm4", 12,),
+    ("quant_w8", 512, 256,),
+    ("silu", 9,),
+    ("add", 8,),
+    ("store_res", 0, 0, 4, 256, 256,),
+    ("mm4", 14,),
+    ("silu", 10,),
+    ("add", 11,),
+    ("mm8", 13,),
+    ("mm8", 12,),
+    ("silu", 8,),
+    ("add", 13,),
+    ("mm8", 14,),
+    ("mm4", 15,),
+    ("silu", 11,),
+    ("add", 12,),
+    ("store_res", 1, 0, 2, 0, 512,),
+    ("mm8", 15,),
+    ("silu", 13,),
+    ("add", 14,),
+    ("store_res", 1, 2, 4, 0, 512,),
+    ("mm4", 16,),
+    ("mm8", 16,),
+    ("silu", 12,),
+    ("cast_res", "V", 1, 256, 256,),
+    ("mm4", 19,),
+    ("cast_res", "S", 1, 0, 256,),
+    ("mm8", 19,),
+    ("store_res", 0, 0, 2, 512, 512,),
+    ("add", 15,),
+    ("mm4", 17,),
+    ("add", 16,),
+    ("mm8", 17,),
+    ("silu", 14,),
+    ("quant_res", 1, 256, 256,),
     ("quant_res", 1, 0, 256,),
-    ("store_res", 3, 0, 2,),
-    ("mm4", 4, 2,),
-    ("add", 3, 3,),
-    ("mm8", 4, 2,),
-    ("silu", 3, 2, 3,),
-    ("mm8", 4, 1,),
-    ("store_codes", 0, 0, 512,),
-    ("add", 4, 3,),
-    ("silu", 4, 0, 1,),
-    ("silu", 3, 3, 4,),
-    ("add", 4, 2,),
-    ("silu", 4, 3, 4,),
-    ("add", 4, 1,),
-    ("store_res", 3, 2, 4,),
-    ("silu", 4, 2, 3,),
-    ("cast_res", "V", 3, 0, 128,),
-    ("silu", 4, 1, 2,),
-    ("cast_res", "V", 3, 256, 384,),
-    ("store_res", 4, 2, 4,),
-    ("cast_res", "V", 2, 384, 512,),
-    ("cast_res", "V", 3, 128, 256,),
-    ("cast_res", "S", 3, 384, 512,),
-    ("cast_res", "V", 2, 0, 128,),
-    ("quant_res", 3, 0, 256,),
-    ("cast_res", "S", 2, 256, 384,),
-    ("cast_res", "V", 4, 256, 384,),
-    ("quant_res", 2, 0, 256,),
-    ("cast_res", "S", 4, 128, 256,),
-    ("quant_res", 3, 256, 512,),
-    ("cast_res", "V", 4, 384, 512,),
-    ("store_res", 4, 0, 2,),
-    ("cast_res", "S", 4, 0, 128,),
-    ("store_codes", 0, 512, 512,),
-    ("quant_res", 2, 256, 512,),
+    ("silu", 15,),
+    ("mm4", 18,),
+    ("mm8", 18,),
+    ("add", 17,),
     ("store_codes", 1, 0, 512,),
-    ("quant_res", 4, 256, 512,),
-    ("quant_res", 4, 0, 256,),
-    ("store_scales", "SP", 3,),
-    ("store_scales", "S", 2,),
-    ("store_scales", "S", 0,),
-    ("store_scales", "SP", 1,),
+    ("cast_res", "S", 0, 128, 128,),
+    ("store_res", 0, 2, 4, 512, 512,),
+    ("add", 18,),
+    ("silu", 16,),
+    ("add", 19,),
+    ("silu", 17,),
+    ("cast_res", "V", 0, 512, 256,),
+    ("silu", 18,),
+    ("store_res", 1, 0, 2, 512, 512,),
+    ("cast_res", "V", 0, 384, 128,),
+    ("silu", 19,),
+    ("cast_res", "V", 0, 768, 256,),
+    ("cast_res", "S", 0, 256, 128,),
+    ("store_res", 1, 2, 4, 512, 512,),
+    ("quant_res", 0, 0, 256,),
+    ("quant_res", 0, 512, 256,),
+    ("cast_res", "S", 1, 768, 256,),
+    ("quant_res", 0, 768, 256,),
+    ("quant_res", 0, 256, 256,),
+    ("cast_res", "V", 1, 512, 256,),
+    ("store_scales", "SP", 0, 0, 1,),
+    ("store_scales", "SP", 2, 0, 1,),
+    ("store_codes", 0, 0, 1024,),
+    ("store_scales", "SP", 1, 0, 1,),
+    ("quant_res", 1, 768, 256,),
+    ("quant_res", 1, 512, 256,),
     ("store_codes", 1, 512, 512,),
+    ("store_scales", "SP", 1, 1, 2,),
+    ("store_scales", "SP", 3, 0, 1,),
+    ("store_scales", "SP", 3, 1, 2,),
+    ("store_scales", "S", 2, 1, 2,),
+    ("store_scales", "S", 0, 1, 2,),
 ]
 
 
@@ -192,182 +200,27 @@ def tile_mix_atom_tm_pl_silu_kernel(
 
         banks = [ps.tile([P, 512], F32, name="bank%d" % i) for i in range(8)]
 
-        x4_raw = [tile("x4_raw%d" % a, [P, G4, 2 * HALF], U8) for a in range(2)]
+        chunks = {"x4": {}, "w4": {}, "x8": {}, "w8": {}}
         xs_raw = tile("xs_raw", [P, G4, T], U8)
-        x4_dealt = [tile("x4_dealt%d" % a, [P, G4, PACK, 2 * P], U8) for a in range(2)]
+        x4_dealt = [[tile("x4_dealt%d_%d" % (a, g), [P, PACK, 2 * P], U8) for g in range(G4)] for a in range(2)]
         xs_dealt = [tile("xs_dealt%d" % a, [P, G4, PACK, P], U8) for a in range(2)]
-        w4 = [tile("w4_%d" % h, [P, G4, 2 * HALF], U8) for h in range(2)]
         ws = tile("ws", [P, G4, M], U8)
-        x8_raw = [tile("x8_raw%d" % a, [P, PACK, HALF], F32) for a in range(2)]
         x8_bf = [[tile("x8_bf%d_%d" % (a, s), [P, 2, P, PACK], BF16) for s in range(2)] for a in range(2)]
         x8_codes = [tile("x8_codes%d" % a, [P, PACK * P], U32) for a in range(2)]
         x8_scales = [tile("x8_scales%d" % a, [P, PACK * P], U8) for a in range(2)]
         w8_codes = tile("w8_codes", [P, M], U32)
         w8_scales = tile("w8_scales", [P, M], U8)
-        w8_raw = {}
         w8_bf = tile("w8_bf", [P, M, PACK], BF16)
-        b_rows = tile("b_rows", [P, 8], F32)
+        b_rows = tile("b_rows", [P, P], F32)
+        b_cols = tile("b_cols", [P, 8], F32)
         ident = tile("ident", [P, P], F32)
         bias = tile("bias", [P, M], F32)
         warm = tile("warm", [P, 8], F32)
-        res = [tile("res%d" % u, [P, PACK, UNITS[u][2]], F32) for u in range(len(UNITS))]
-        pre = [tile("pre%d" % u, [P, PACK, UNITS[u][2]], F32) for u in range(len(UNITS))]
-        res_bf = [tile("res_bf%d" % u, [P, UNITS[u][2], PACK], BF16) for u in range(len(UNITS))]
+        res = {(a, n0): tile("res%d_%d" % (a, n0), [P, PACK, width], F32) for a, n0, width in RES}
+        pre = [tile("pre%d" % u, [P, UNITS[u][6]], F32) for u in range(len(UNITS))]
+        res_bf = [tile("res_bf%d" % a, [P, M, PACK], BF16) for a in range(2)]
         out_codes = tile("out_codes", [P, 2, M], U32)
         out_scales = tile("out_scales", [P, 2, M], U8)
-
-        def interleave(eng, dst, src):
-            cast(eng, dst.rearrange("p (c i) j -> p c j i", i=4), src.rearrange("p j (c i) -> p c j i", i=4))
-
-        def load_scales(queue, plane, scales):
-            for q in range(4):
-                queue.dma_start(
-                    out=plane[32 * q : 32 * q + 4, :, :].bitcast(I32),
-                    in_=scales[:, 4 * q : 4 * q + 4, :].rearrange("g r n -> r g n").bitcast(I32),
-                )
-
-        def load_x4(a):
-            nc.sync.dma_start(
-                out=x4_raw[a][:].bitcast(I32),
-                in_=x4_words[:, :, 2 * HALF * a : 2 * HALF * (a + 1)].rearrange("g p c -> p g c").bitcast(I32),
-            )
-
-        def load_w4(h):
-            nc.sync.dma_start(
-                out=w4[h][:].bitcast(I32),
-                in_=w4_words[:, :, 2 * HALF * h : 2 * HALF * (h + 1)].rearrange("g p c -> p g c").bitcast(I32),
-            )
-
-        def load_w8(n0, width):
-            raw = tile("w8_raw%d" % n0, [P, PACK, width], F32)
-            w8_raw[n0] = raw
-            nc.sync.dma_start(out=raw[:], in_=w8[:, n0 : n0 + width].rearrange("(p j) n -> p j n", j=PACK))
-
-        def load_x8(a):
-            nc.sync.dma_start(
-                out=x8_raw[a][:], in_=x8[:, HALF * a : HALF * (a + 1)].rearrange("(p j) t -> p j t", j=PACK)
-            )
-
-        def bias_tr():
-            for e in range(8):
-                nc.tensor.transpose(
-                    banks[6 + e // 4][:, P * (e % 4) : P * (e % 4 + 1)],
-                    b_rows[:, e : e + 1].to_broadcast([P, P]),
-                    ident[:],
-                )
-
-        def bias_cp(half):
-            nc.scalar.copy(
-                out=bias[:].rearrange("p (m e) -> p m e", e=8)[:, :, 4 * half : 4 * half + 4],
-                in_=banks[6 + half][:].rearrange("p (e m) -> p m e", e=4),
-            )
-
-        def deal_x4(a, g):
-            nc.vector.tensor_copy(
-                out=x4_dealt[a][:, g].rearrange("p r (m y) -> p r m y", y=2),
-                in_=x4_raw[a][:, g, :].rearrange("p (m r y) -> p r m y", r=PACK, y=2),
-            )
-
-        def deal_xs(a):
-            nc.vector.tensor_copy(
-                out=xs_dealt[a][:],
-                in_=xs_raw[:, :, HALF * a : HALF * (a + 1)].rearrange("p g (m r) -> p g r m", r=PACK),
-            )
-
-        def cast_x8(eng, a, s):
-            cast(
-                eng,
-                x8_bf[a][s][:].rearrange("p r m j -> p m j r"),
-                x8_raw[a][:].rearrange("p j (m r) -> p m j r", r=PACK)[:, :, :, 2 * s : 2 * s + 2],
-            )
-
-        def quant_x8(a, s):
-            cols = slice(2 * P * s, 2 * P * (s + 1))
-            nc.vector.quantize_mx(
-                out=x8_codes[a][:, cols].bitcast(FP8X4),
-                scales=x8_scales[a][:, cols],
-                in_=x8_bf[a][s][:].rearrange("p r m j -> p (r m j)"),
-            )
-
-        def cast_w8(eng, n0, width):
-            first = max(c for c in w8_raw if c <= n0)
-            interleave(eng, w8_bf[:, n0 : n0 + width, :], w8_raw[first][:, :, n0 - first : n0 - first + width])
-
-        def quant_w8(n0, width):
-            nc.vector.quantize_mx(
-                out=w8_codes[:, n0 : n0 + width].bitcast(FP8X4),
-                scales=w8_scales[:, n0 : n0 + width],
-                in_=w8_bf[:, n0 : n0 + width, :].rearrange("p c j -> p (c j)"),
-            )
-
-        def bank_of(u, r):
-            return banks[4 * (u % 2) + r][:, 0 : UNITS[u][2]]
-
-        def mm4(u, r):
-            a, n0, width = UNITS[u]
-            h, c0 = divmod(n0, HALF)
-            for g in range(G4):
-                nc.tensor.matmul_mx(
-                    out=bank_of(u, r),
-                    lhsT=x4_dealt[a][:, g, r, :].bitcast(FP4X4),
-                    lhsT_scale=xs_dealt[a][:, g, r, :],
-                    rhs=w4[h][:, g, 2 * c0 : 2 * (c0 + width)].bitcast(FP4X4),
-                    rhs_scale=ws[:, g, n0 : n0 + width],
-                    start=(g == 0),
-                    stop=False,
-                )
-
-        def mm8(u, r):
-            a, n0, width = UNITS[u]
-            nc.tensor.matmul_mx(
-                out=bank_of(u, r),
-                lhsT=x8_codes[a][:, P * r : P * (r + 1)].bitcast(FP8X4),
-                lhsT_scale=x8_scales[a][:, P * r : P * (r + 1)],
-                rhs=w8_codes[:, n0 : n0 + width].bitcast(FP8X4),
-                rhs_scale=w8_scales[:, n0 : n0 + width],
-                start=False,
-                stop=True,
-            )
-
-        def add_bias(u, r):
-            a, n0, width = UNITS[u]
-            nc.vector.tensor_tensor(out=pre[u][:, r, :], in0=bank_of(u, r), in1=bias[:, n0 : n0 + width], op=ADD)
-
-        def res_of(u):
-            return res[u][:]
-
-        def silu(u, r0, r1):
-            nc.scalar.activation(out=res_of(u)[:, r0:r1, :], in_=pre[u][:, r0:r1, :], func=SILU)
-
-        def cast_res(eng, u, c0, c1):
-            interleave(eng, res_bf[u][:, c0:c1, :], res_of(u)[:, :, c0:c1])
-
-        def quant_res(u, c0, c1):
-            a, n0, width = UNITS[u]
-            nc.vector.quantize_mx(
-                out=out_codes[:, a, n0 + c0 : n0 + c1].bitcast(FP8X4),
-                scales=out_scales[:, a, n0 + c0 : n0 + c1],
-                in_=res_bf[u][:, c0:c1, :].rearrange("p c j -> p (c j)"),
-            )
-
-        def store_res(u, r0, r1):
-            a, n0, width = UNITS[u]
-            nc.sync.dma_start(
-                out=out_0[HALF * a : HALF * (a + 1), n0 : n0 + width].rearrange("(p r) n -> p r n", r=PACK)[:, r0:r1, :],
-                in_=res[u][:, r0:r1, :],
-            )
-
-        def store_codes(a, n0, width):
-            nc.sync.dma_start(
-                out=out_1[a].rearrange("p n i -> p (n i)").bitcast(I32)[:, n0 : n0 + width],
-                in_=out_codes[:, a, n0 : n0 + width].bitcast(I32),
-            )
-
-        def store_scales(queue, q):
-            queue.dma_start(
-                out=out_2[:, 4 * q : 4 * q + 4, :].rearrange("g r n -> r g n").bitcast(I32),
-                in_=out_scales[32 * q : 32 * q + 4, :, :].bitcast(I32),
-            )
 
         def cast(eng, dst, src):
             if eng == "V":
@@ -377,24 +230,207 @@ def tile_mix_atom_tm_pl_silu_kernel(
             else:
                 nc.gpsimd.tensor_scalar(out=dst, in0=src, scalar1=1.0, scalar2=0.0, op0=MULT, op1=ADD)
 
+        def interleave(eng, dst, src):
+            cast(eng, dst.rearrange("p (c i) j -> p c j i", i=4), src.rearrange("p j (c i) -> p c j i", i=4))
+
+        def cols(kind, c0, width, per=1):
+            first = max(c for c in chunks[kind] if c <= c0)
+            return chunks[kind][first][:, :, per * (c0 - first) : per * (c0 - first + width)]
+
+        def res_cols(a, c0, width):
+            first = max(n0 for aa, n0 in res if aa == a and n0 <= c0)
+            return res[(a, first)][:, :, c0 - first : c0 - first + width]
+
+        def load_scales(queue, plane, scales):
+            for r in range(4):
+                queue.dma_start(
+                    out=plane[r:P:32, :, :].bitcast(I32),
+                    in_=scales.rearrange("g (q r) n -> r q g n", r=4)[r].bitcast(I32),
+                )
+
+        def load4(kind, c0, width):
+            words = x4_words if kind == "x4" else w4_words
+            raw = tile("%s_raw%d" % (kind, c0), [P, G4, 2 * width], U8)
+            chunks[kind][c0] = raw
+            nc.sync.dma_start(
+                out=raw[:].bitcast(I32),
+                in_=words[:, :, 2 * c0 : 2 * (c0 + width)].rearrange("g p c -> p g c").bitcast(I32),
+            )
+
+        def load8(kind, c0, width):
+            src = x8 if kind == "x8" else w8
+            raw = tile("%s_raw%d" % (kind, c0), [P, PACK, width], F32)
+            chunks[kind][c0] = raw
+            nc.sync.dma_start(out=raw[:], in_=src[:, c0 : c0 + width].rearrange("(p j) n -> p j n", j=PACK))
+
+        def bcol_tr():
+            nc.tensor.transpose(banks[BB[0]][:, 0:P], b_rows[:], ident[:])
+
+        def bcol_cp():
+            nc.scalar.copy(out=b_cols[:], in_=banks[BB[0]][:, 0:8])
+
+        def bias_tr(half):
+            for e in range(4):
+                c = 4 * half + e
+                nc.tensor.transpose(
+                    banks[BB[1 + half]][:, P * e : P * (e + 1)], b_cols[:, c : c + 1].to_broadcast([P, P]), ident[:]
+                )
+
+        def bias_cp(half):
+            nc.scalar.copy(out=bias[:, HALF * half : HALF * (half + 1)], in_=banks[BB[1 + half]][:])
+
+        def deal_x4(a, g):
+            nc.vector.tensor_copy(
+                out=x4_dealt[a][g][:].rearrange("p r (m y) -> p r m y", y=2),
+                in_=cols("x4", HALF * a, HALF, 2)[:, g, :].rearrange("p (m r y) -> p r m y", r=PACK, y=2),
+            )
+
+        def deal_xs(a):
+            nc.vector.tensor_copy(
+                out=xs_dealt[a][:],
+                in_=xs_raw[:, :, HALF * a : HALF * (a + 1)].rearrange("p g (m r) -> p g r m", r=PACK),
+            )
+
+        def cast_x8(eng, a, s):
+            if a in DEALT:
+                cast(
+                    eng,
+                    x8_bf[a][s][:].rearrange("p r m j -> p m j r"),
+                    cols("x8", HALF * a, HALF).rearrange("p j (m r) -> p m j r", r=PACK)[:, :, :, 2 * s : 2 * s + 2],
+                )
+            else:
+                interleave(eng, x8_bf[a][s][:].rearrange("p r m j -> p (r m) j"), cols("x8", HALF * a + 256 * s, 256))
+
+        def quant_x8(a, s):
+            span = slice(2 * P * s, 2 * P * (s + 1))
+            nc.vector.quantize_mx(
+                out=x8_codes[a][:, span].bitcast(FP8X4),
+                scales=x8_scales[a][:, span],
+                in_=x8_bf[a][s][:].rearrange("p r m j -> p (r m j)"),
+            )
+
+        def cast_w8(eng, n0, width):
+            interleave(eng, w8_bf[:, n0 : n0 + width, :], cols("w8", n0, width))
+
+        def quant_w8(n0, width):
+            nc.vector.quantize_mx(
+                out=w8_codes[:, n0 : n0 + width].bitcast(FP8X4),
+                scales=w8_scales[:, n0 : n0 + width],
+                in_=w8_bf[:, n0 : n0 + width, :].rearrange("p c j -> p (c j)"),
+            )
+
+        def mm4(u):
+            kind, a, i, n0, bank, first, width = UNITS[u]
+            for g in range(G4):
+                if kind == "A":
+                    x, xs = x4_dealt[a][g][:, i, :], xs_dealt[a][:, g, i, :]
+                    w, wsc = cols("w4", n0, width, 2)[:, g, :], ws[:, g, n0 : n0 + width]
+                    ops = (x, xs, w, wsc)
+                else:
+                    x, xs = cols("x4", HALF * a, HALF, 2)[:, g, :], xs_raw[:, g, HALF * a : HALF * (a + 1)]
+                    w, wsc = cols("w4", n0, P, 2)[:, g, :], ws[:, g, n0 : n0 + P]
+                    ops = (w, wsc, x, xs)
+                nc.tensor.matmul_mx(
+                    out=banks[bank][:, 0:width],
+                    lhsT=ops[0].bitcast(FP4X4),
+                    lhsT_scale=ops[1],
+                    rhs=ops[2].bitcast(FP4X4),
+                    rhs_scale=ops[3],
+                    start=(g == 0 and first == 4),
+                    stop=(g == G4 - 1 and first == 8),
+                )
+
+        def mm8(u):
+            kind, a, i, n0, bank, first, width = UNITS[u]
+            if kind == "A":
+                ops = (x8_codes[a][:, P * i : P * (i + 1)], x8_scales[a][:, P * i : P * (i + 1)],
+                       w8_codes[:, n0 : n0 + width], w8_scales[:, n0 : n0 + width])
+            else:
+                ops = (w8_codes[:, n0 : n0 + P], w8_scales[:, n0 : n0 + P], x8_codes[a][:], x8_scales[a][:])
+            nc.tensor.matmul_mx(
+                out=banks[bank][:, 0:width],
+                lhsT=ops[0].bitcast(FP8X4),
+                lhsT_scale=ops[1],
+                rhs=ops[2].bitcast(FP8X4),
+                rhs_scale=ops[3],
+                start=(first == 8),
+                stop=(first == 4),
+            )
+
+        def add_bias(u):
+            kind, a, i, n0, bank, first, width = UNITS[u]
+            nc.vector.tensor_tensor(out=pre[u][:], in0=banks[bank][:, 0:width], in1=bias[:, n0 : n0 + width], op=ADD)
+
+        def silu(u):
+            kind, a, i, n0, bank, first, width = UNITS[u]
+            if kind == "A":
+                nc.scalar.activation(out=res_cols(a, n0, width)[:, i, :], in_=pre[u][:], func=SILU)
+            else:
+                nc.scalar.activation(
+                    out=pre[u][:].rearrange("p (r m) -> p r m", r=PACK),
+                    in_=banks[bank][:].rearrange("p (m r) -> p r m", r=PACK),
+                    func=SILU,
+                    bias=b_cols[:, n0 // P : n0 // P + 1],
+                )
+
+        def turn(u):
+            kind, a, i, n0, bank, first, width = UNITS[u]
+            for r in range(PACK):
+                nc.tensor.transpose(banks[i][:, P * r : P * (r + 1)], pre[u][:, P * r : P * (r + 1)], ident[:])
+
+        def cast_out(eng, u):
+            kind, a, i, n0, bank, first, width = UNITS[u]
+            cast(eng, res_cols(a, n0, P), banks[i][:].rearrange("p (r n) -> p r n", r=PACK))
+
+        def cast_res(eng, a, c0, width):
+            interleave(eng, res_bf[a][:, c0 : c0 + width, :], res_cols(a, c0, width))
+
+        def quant_res(a, c0, width):
+            nc.vector.quantize_mx(
+                out=out_codes[:, a, c0 : c0 + width].bitcast(FP8X4),
+                scales=out_scales[:, a, c0 : c0 + width],
+                in_=res_bf[a][:, c0 : c0 + width, :].rearrange("p c j -> p (c j)"),
+            )
+
+        def store_res(a, r0, r1, n0, width):
+            nc.sync.dma_start(
+                out=out_0[HALF * a : HALF * (a + 1), n0 : n0 + width].rearrange("(p r) n -> p r n", r=PACK)[:, r0:r1, :],
+                in_=res_cols(a, n0, width)[:, r0:r1, :],
+            )
+
+        def store_codes(a, n0, width):
+            nc.sync.dma_start(
+                out=out_1[a].rearrange("p n i -> p (n i)").bitcast(I32)[:, n0 : n0 + width],
+                in_=out_codes[:, a, n0 : n0 + width].bitcast(I32),
+            )
+
+        def store_scales(queue, r, a0, a1):
+            queue.dma_start(
+                out=out_2.rearrange("g (q r) n -> r q g n", r=4)[r][:, a0:a1, :].bitcast(I32),
+                in_=out_scales[r:P:32, a0:a1, :].bitcast(I32),
+            )
+
         def setup():
             nc.vector.memset(xs_raw[:].rearrange("p g t -> p (g t)").bitcast(I32), 0)
             nc.vector.memset(ws[:].rearrange("p g t -> p (g t)").bitcast(I32), 0)
             nc.vector.memset(warm[:, 0:1], 0.0)
-            nc.gpsimd.dma_start(out=b_rows[:], in_=b.rearrange("(p e) -> p e", e=8))
+            nc.gpsimd.memset(b_rows[:], 0.0)
+            nc.gpsimd.dma_start(out=b_rows[0:8, :], in_=b.rearrange("(c p) -> c p", p=P))
             make_identity(nc, ident[:])
             nc.scalar.activation(out=warm[:, 1:2], in_=warm[:, 0:1], func=SILU)
 
         queues = {"SP": nc.sync, "S": nc.scalar}
         table = {
             "setup": setup,
-            "load_x4": load_x4,
             "load_xs": lambda e: load_scales(queues[e], xs_raw, x4_scales),
             "load_ws": lambda e: load_scales(queues[e], ws, w4_scales),
-            "load_w4": load_w4,
-            "load_w8": load_w8,
-            "load_x8": load_x8,
+            "load4": load4,
+            "load8": load8,
             "bias_tr": bias_tr,
+            "bcol_tr": bcol_tr,
+            "bcol_cp": bcol_cp,
+            "turn": turn,
+            "cast_out": cast_out,
             "bias_cp": bias_cp,
             "deal_x4": deal_x4,
             "deal_xs": deal_xs,
@@ -410,7 +446,7 @@ def tile_mix_atom_tm_pl_silu_kernel(
             "quant_res": quant_res,
             "store_res": store_res,
             "store_codes": store_codes,
-            "store_scales": lambda e, q: store_scales(queues[e], q),
+            "store_scales": lambda e, r, a0, a1: store_scales(queues[e], r, a0, a1),
         }
         for step in STEPS:
             table[step[0]](*step[1:])

@@ -30,159 +30,156 @@ STEPS = [
     ("setup",),
     ("load4", "x4", 0, 1024,),
     ("load_xs", "SP",),
-    ("load4", "w4", 0, 512,),
+    ("load8", "w8", 0, 256,),
     ("load8", "x8", 0, 512,),
     ("deal_x4", 1, 0,),
     ("load_ws", "SP",),
-    ("load8", "w8", 0, 256,),
-    ("bcol_tr",),
-    ("deal_xs", 0,),
-    ("load8", "w8", 256, 256,),
-    ("bcol_cp",),
-    ("deal_x4", 1, 1,),
-    ("load8", "x8", 512, 512,),
-    ("bias_tr", 1,),
-    ("deal_xs", 1,),
+    ("load4", "w4", 0, 512,),
     ("deal_x4", 0, 0,),
-    ("bias_tr", 0,),
     ("deal_x4", 0, 1,),
-    ("mm4", 3,),
-    ("cast_x8", "S", 0, 0,),
-    ("cast_x8", "V", 0, 1,),
+    ("deal_xs", 0,),
+    ("load_b", "S",),
+    ("bcol_tr",),
+    ("cast_w8", "S", 0, 256,),
+    ("bcol_cp",),
+    ("quant_w8", 0, 256,),
+    ("load8", "w8", 256, 256,),
+    ("bias_tr", 1,),
+    ("cast_x8", "S", 0, 1,),
+    ("cast_x8", "V", 0, 0,),
+    ("load8", "x8", 512, 512,),
+    ("bias_tr", 0,),
     ("load8", "w8", 512, 512,),
     ("load4", "w4", 512, 512,),
+    ("deal_x4", 1, 1,),
+    ("bias_cp", 1,),
+    ("quant_x8", 0, 0,),
     ("quant_x8", 0, 1,),
     ("bias_cp", 0,),
-    ("quant_x8", 0, 0,),
-    ("mm4", 2,),
-    ("bias_cp", 1,),
-    ("cast_w8", "V", 0, 256,),
-    ("mm4", 0,),
     ("mm4", 1,),
-    ("quant_w8", 0, 256,),
-    ("cast_w8", "V", 256, 256,),
-    ("mm8", 3,),
-    ("mm8", 2,),
+    ("deal_xs", 1,),
+    ("mm4", 2,),
     ("mm8", 1,),
-    ("mm8", 0,),
-    ("add", 2,),
-    ("mm4", 6,),
-    ("quant_w8", 256, 256,),
-    ("mm4", 7,),
-    ("silu", 2,),
-    ("add", 3,),
-    ("mm4", 5,),
-    ("mm8", 7,),
-    ("add", 0,),
-    ("mm4", 4,),
-    ("silu", 3,),
+    ("mm8", 2,),
+    ("cast_w8", "S", 256, 256,),
     ("add", 1,),
-    ("mm8", 4,),
-    ("mm8", 5,),
-    ("silu", 0,),
-    ("add", 7,),
+    ("add", 2,),
+    ("mm4", 0,),
+    ("mm8", 0,),
+    ("add", 0,),
+    ("mm4", 3,),
+    ("mm8", 3,),
+    ("silu", 2,),
+    ("mm4", 5,),
+    ("quant_w8", 256, 256,),
     ("silu", 1,),
-    ("mm4", 11,),
-    ("cast_x8", "V", 1, 1,),
-    ("cast_x8", "S", 1, 0,),
-    ("mm8", 6,),
-    ("store_res", 0, 0, 4, 0, 256,),
-    ("mm4", 8,),
-    ("add", 4,),
-    ("quant_x8", 1, 1,),
+    ("add", 3,),
+    ("silu", 0,),
     ("mm4", 10,),
+    ("cast_x8", "V", 1, 0,),
+    ("cast_x8", "S", 1, 1,),
+    ("mm4", 6,),
+    ("mm8", 5,),
+    ("mm8", 6,),
+    ("mm4", 4,),
+    ("mm8", 4,),
     ("add", 5,),
-    ("cast_res", "S", 0, 0, 128,),
-    ("mm8", 10,),
+    ("mm4", 11,),
     ("add", 6,),
-    ("mm8", 11,),
-    ("quant_x8", 1, 0,),
+    ("silu", 3,),
+    ("add", 4,),
+    ("mm4", 7,),
+    ("mm8", 7,),
     ("silu", 5,),
-    ("add", 10,),
-    ("silu", 4,),
-    ("mm4", 9,),
-    ("cast_w8", "S", 512, 256,),
-    ("mm8", 9,),
-    ("cast_w8", "V", 768, 256,),
-    ("mm8", 8,),
-    ("add", 9,),
-    ("mm4", 13,),
+    ("quant_x8", 1, 0,),
+    ("store_res", 0, 0, 4, 0, 256,),
     ("silu", 6,),
+    ("mm4", 9,),
+    ("quant_x8", 1, 1,),
+    ("silu", 4,),
+    ("cast_res", "V", 0, 128, 128,),
+    ("add", 7,),
+    ("cast_w8", "S", 512, 256,),
+    ("cast_w8", "V", 768, 256,),
+    ("mm8", 9,),
+    ("mm4", 8,),
+    ("mm8", 10,),
+    ("mm8", 11,),
+    ("add", 9,),
     ("quant_w8", 768, 256,),
+    ("mm8", 8,),
     ("silu", 7,),
-    ("mm4", 12,),
-    ("quant_w8", 512, 256,),
-    ("silu", 9,),
-    ("add", 8,),
-    ("store_res", 0, 0, 4, 256, 256,),
-    ("mm4", 14,),
-    ("silu", 10,),
-    ("add", 11,),
-    ("mm8", 13,),
-    ("mm8", 12,),
-    ("silu", 8,),
-    ("add", 13,),
-    ("mm8", 14,),
     ("mm4", 15,),
-    ("silu", 11,),
-    ("add", 12,),
-    ("store_res", 1, 0, 2, 0, 512,),
+    ("store_res", 0, 0, 4, 256, 256,),
+    ("cast_res", "S", 0, 0, 128,),
+    ("mm4", 14,),
+    ("quant_w8", 512, 256,),
     ("mm8", 15,),
-    ("silu", 13,),
+    ("add", 8,),
+    ("cast_res", "S", 0, 384, 128,),
+    ("silu", 9,),
+    ("mm8", 14,),
+    ("add", 11,),
+    ("mm4", 17,),
+    ("add", 10,),
+    ("silu", 8,),
     ("add", 14,),
-    ("store_res", 1, 2, 4, 0, 512,),
+    ("silu", 11,),
+    ("mm8", 17,),
     ("mm4", 16,),
     ("mm8", 16,),
-    ("silu", 12,),
-    ("cast_res", "V", 1, 256, 256,),
-    ("mm4", 19,),
-    ("cast_res", "S", 1, 0, 256,),
-    ("mm8", 19,),
-    ("store_res", 0, 0, 2, 512, 512,),
     ("add", 15,),
-    ("mm4", 17,),
-    ("add", 16,),
-    ("mm8", 17,),
-    ("silu", 14,),
-    ("quant_res", 1, 256, 256,),
-    ("quant_res", 1, 0, 256,),
-    ("silu", 15,),
-    ("mm4", 18,),
-    ("mm8", 18,),
+    ("store_res", 1, 0, 2, 0, 512,),
+    ("silu", 10,),
     ("add", 17,),
-    ("store_codes", 1, 0, 512,),
-    ("cast_res", "S", 0, 128, 128,),
-    ("store_res", 0, 2, 4, 512, 512,),
-    ("add", 18,),
+    ("silu", 14,),
+    ("store_res", 1, 2, 4, 0, 512,),
+    ("mm4", 13,),
+    ("add", 16,),
+    ("mm8", 13,),
+    ("mm4", 12,),
+    ("mm8", 12,),
+    ("silu", 15,),
+    ("cast_res", "V", 1, 256, 256,),
+    ("cast_res", "S", 0, 256, 128,),
     ("silu", 16,),
-    ("add", 19,),
+    ("mm4", 18,),
+    ("add", 13,),
+    ("mm8", 18,),
+    ("add", 12,),
     ("silu", 17,),
-    ("cast_res", "V", 0, 512, 256,),
-    ("silu", 18,),
+    ("mm4", 19,),
+    ("store_res", 0, 2, 4, 512, 512,),
+    ("mm8", 19,),
+    ("quant_res", 0, 0, 256,),
+    ("silu", 13,),
+    ("add", 18,),
     ("store_res", 1, 0, 2, 512, 512,),
-    ("cast_res", "V", 0, 384, 128,),
+    ("silu", 12,),
+    ("add", 19,),
+    ("quant_res", 0, 256, 256,),
+    ("silu", 18,),
+    ("store_res", 0, 0, 2, 512, 512,),
     ("silu", 19,),
     ("cast_res", "V", 0, 768, 256,),
-    ("cast_res", "S", 0, 256, 128,),
-    ("store_res", 1, 2, 4, 512, 512,),
-    ("quant_res", 0, 0, 256,),
-    ("quant_res", 0, 512, 256,),
+    ("cast_res", "S", 1, 0, 256,),
     ("cast_res", "S", 1, 768, 256,),
+    ("cast_res", "V", 0, 512, 256,),
+    ("store_res", 1, 2, 4, 512, 512,),
     ("quant_res", 0, 768, 256,),
-    ("quant_res", 0, 256, 256,),
+    ("quant_res", 0, 512, 256,),
     ("cast_res", "V", 1, 512, 256,),
-    ("store_scales", "SP", 0, 0, 1,),
-    ("store_scales", "SP", 2, 0, 1,),
     ("store_codes", 0, 0, 1024,),
-    ("store_scales", "SP", 1, 0, 1,),
-    ("quant_res", 1, 768, 256,),
+    ("quant_res", 1, 256, 256,),
+    ("quant_res", 1, 0, 256,),
+    ("store_codes", 1, 0, 512,),
     ("quant_res", 1, 512, 256,),
+    ("quant_res", 1, 768, 256,),
     ("store_codes", 1, 512, 512,),
-    ("store_scales", "SP", 1, 1, 2,),
-    ("store_scales", "SP", 3, 0, 1,),
-    ("store_scales", "SP", 3, 1, 2,),
-    ("store_scales", "S", 2, 1, 2,),
-    ("store_scales", "S", 0, 1, 2,),
+    ("store_scales", "S", 0, 0, 2,),
+    ("store_scales", "SP", 1, 0, 2,),
+    ("store_scales", "SP", 3, 0, 2,),
+    ("store_scales", "S", 2, 0, 2,),
 ]
 
 
@@ -228,7 +225,7 @@ def tile_mix_atom_tm_pl_silu_kernel(
             elif eng == "S":
                 nc.scalar.copy(out=dst, in_=src)
             else:
-                nc.gpsimd.tensor_scalar(out=dst, in0=src, scalar1=1.0, scalar2=0.0, op0=MULT, op1=ADD)
+                nc.gpsimd.tensor_scalar(out=dst, in0=src, scalar1=1.0, scalar2=-0.0, op0=MULT, op1=ADD)
 
         def interleave(eng, dst, src):
             cast(eng, dst.rearrange("p (c i) j -> p c j i", i=4), src.rearrange("p j (c i) -> p c j i", i=4))
@@ -412,16 +409,20 @@ def tile_mix_atom_tm_pl_silu_kernel(
 
         def setup():
             nc.vector.memset(xs_raw[:].rearrange("p g t -> p (g t)").bitcast(I32), 0)
+            nc.vector.memset(warm[:, 1:2], 0.0)
+            nc.vector.memset(b_rows[:], 0.0)
+            nc.vector.memset(ident[:], 0.0)
             nc.vector.memset(ws[:].rearrange("p g t -> p (g t)").bitcast(I32), 0)
-            nc.vector.memset(warm[:, 0:1], 0.0)
-            nc.gpsimd.memset(b_rows[:], 0.0)
-            nc.gpsimd.dma_start(out=b_rows[0:8, :], in_=b.rearrange("(c p) -> c p", p=P))
-            make_identity(nc, ident[:])
-            nc.scalar.activation(out=warm[:, 1:2], in_=warm[:, 0:1], func=SILU)
+            make_identity(nc, ident[:], nomemset=True)
+            nc.scalar.activation(out=warm[:, 0:1], in_=warm[:, 1:2], func=SILU)
+
+        def load_b(e):
+            queues[e].dma_start(out=b_rows[0:8, :], in_=b.rearrange("(c p) -> c p", p=P))
 
         queues = {"SP": nc.sync, "S": nc.scalar}
         table = {
             "setup": setup,
+            "load_b": load_b,
             "load_xs": lambda e: load_scales(queues[e], xs_raw, x4_scales),
             "load_ws": lambda e: load_scales(queues[e], ws, w4_scales),
             "load4": load4,

@@ -23,7 +23,7 @@ HALF = 512
 G4 = 2
 
 UNITS = [("A", 0, 0, 0, 0, 4, 256,), ("A", 0, 1, 0, 1, 4, 256,), ("A", 0, 2, 0, 2, 4, 256,), ("A", 0, 3, 0, 3, 4, 256,), ("A", 0, 0, 256, 4, 4, 256,), ("A", 0, 1, 256, 5, 4, 256,), ("A", 0, 2, 256, 6, 4, 256,), ("A", 0, 3, 256, 7, 4, 256,), ("A", 1, 0, 0, 0, 4, 512,), ("A", 1, 1, 0, 1, 4, 512,), ("A", 1, 2, 0, 2, 4, 512,), ("A", 1, 3, 0, 3, 4, 512,), ("A", 0, 0, 512, 4, 4, 512,), ("A", 0, 1, 512, 5, 4, 512,), ("A", 0, 2, 512, 6, 4, 512,), ("A", 0, 3, 512, 7, 4, 512,), ("A", 1, 0, 512, 0, 4, 512,), ("A", 1, 1, 512, 1, 4, 512,), ("A", 1, 2, 512, 2, 4, 512,), ("A", 1, 3, 512, 3, 4, 512,)]
-RES = [(0, 0, 256,), (0, 256, 256,), (1, 0, 512,), (0, 512, 512,), (1, 512, 512,)]
+RES = [(0, 0, 512,), (1, 0, 512,), (0, 512, 512,), (1, 512, 512,)]
 DEALT = [0,1]
 BB = [5,6,7]
 STEPS = [
@@ -31,155 +31,155 @@ STEPS = [
     ("load4", "x4", 0, 1024,),
     ("load_xs", "SP",),
     ("load8", "w8", 0, 256,),
-    ("load8", "x8", 0, 512,),
     ("deal_x4", 1, 0,),
     ("load_ws", "SP",),
     ("load4", "w4", 0, 512,),
-    ("deal_x4", 0, 0,),
-    ("deal_x4", 0, 1,),
-    ("deal_xs", 0,),
-    ("load_b", "S",),
-    ("bcol_tr",),
-    ("cast_w8", "S", 0, 256,),
-    ("bcol_cp",),
-    ("quant_w8", 0, 256,),
+    ("load8", "x8", 0, 512,),
     ("load8", "w8", 256, 256,),
-    ("bias_tr", 1,),
-    ("cast_x8", "S", 0, 1,),
-    ("cast_x8", "V", 0, 0,),
+    ("deal_x4", 0, 0,),
     ("load8", "x8", 512, 512,),
-    ("bias_tr", 0,),
+    ("deal_xs", 0,),
     ("load8", "w8", 512, 512,),
+    ("load_b", "S",),
+    ("cast_w8", "S", 0, 256,),
     ("load4", "w4", 512, 512,),
-    ("deal_x4", 1, 1,),
-    ("bias_cp", 1,),
-    ("quant_x8", 0, 0,),
-    ("quant_x8", 0, 1,),
-    ("bias_cp", 0,),
-    ("mm4", 1,),
-    ("deal_xs", 1,),
-    ("mm4", 2,),
-    ("mm8", 1,),
-    ("mm8", 2,),
-    ("cast_w8", "S", 256, 256,),
-    ("add", 1,),
-    ("add", 2,),
-    ("mm4", 0,),
-    ("mm8", 0,),
-    ("add", 0,),
+    ("deal_x4", 0, 1,),
+    ("quant_w8", 0, 256,),
     ("mm4", 3,),
-    ("mm8", 3,),
-    ("silu", 2,),
+    ("deal_x4", 1, 1,),
+    ("mm4", 4,),
+    ("bcol_tr",),
+    ("deal_xs", 1,),
+    ("bcol_cp",),
+    ("cast_x8", "S", 0, 0,),
+    ("bias_tr", 0,),
+    ("cast_x8", "V", 0, 1,),
+    ("bias_cp", 0,),
+    ("bias_tr", 1,),
+    ("mm4", 0,),
+    ("quant_x8", 0, 1,),
+    ("bias_cp", 1,),
+    ("mm4", 1,),
     ("mm4", 5,),
+    ("cast_w8", "V", 256, 256,),
+    ("mm4", 2,),
+    ("mm8", 2,),
+    ("quant_x8", 0, 0,),
+    ("mm4", 6,),
+    ("mm8", 3,),
     ("quant_w8", 256, 256,),
-    ("silu", 1,),
+    ("mm4", 7,),
+    ("add", 2,),
+    ("mm8", 1,),
+    ("mm8", 0,),
     ("add", 3,),
-    ("silu", 0,),
-    ("mm4", 10,),
+    ("mm8", 6,),
+    ("mm8", 4,),
+    ("silu", 2,),
+    ("add", 1,),
+    ("mm8", 7,),
+    ("mm8", 5,),
+    ("silu", 3,),
     ("cast_x8", "V", 1, 0,),
     ("cast_x8", "S", 1, 1,),
-    ("mm4", 6,),
-    ("mm8", 5,),
-    ("mm8", 6,),
-    ("mm4", 4,),
-    ("mm8", 4,),
-    ("add", 5,),
     ("mm4", 11,),
     ("add", 6,),
-    ("silu", 3,),
-    ("add", 4,),
-    ("mm4", 7,),
-    ("mm8", 7,),
-    ("silu", 5,),
-    ("quant_x8", 1, 0,),
-    ("store_res", 0, 0, 4, 0, 256,),
+    ("mm4", 10,),
+    ("add", 0,),
+    ("add", 7,),
     ("silu", 6,),
     ("mm4", 9,),
+    ("quant_x8", 1, 0,),
+    ("silu", 0,),
     ("quant_x8", 1, 1,),
-    ("silu", 4,),
-    ("cast_res", "V", 0, 128, 128,),
-    ("add", 7,),
-    ("cast_w8", "S", 512, 256,),
-    ("cast_w8", "V", 768, 256,),
-    ("mm8", 9,),
+    ("silu", 1,),
     ("mm4", 8,),
-    ("mm8", 10,),
-    ("mm8", 11,),
-    ("add", 9,),
-    ("quant_w8", 768, 256,),
+    ("add", 4,),
     ("mm8", 8,),
     ("silu", 7,),
-    ("mm4", 15,),
-    ("store_res", 0, 0, 4, 256, 256,),
-    ("cast_res", "S", 0, 0, 128,),
-    ("mm4", 14,),
-    ("quant_w8", 512, 256,),
-    ("mm8", 15,),
+    ("add", 5,),
+    ("cast_w8", "G", 512, 256,),
+    ("mm8", 9,),
+    ("cast_w8", "S", 768, 256,),
     ("add", 8,),
-    ("cast_res", "S", 0, 384, 128,),
-    ("silu", 9,),
-    ("mm8", 14,),
-    ("add", 11,),
-    ("mm4", 17,),
-    ("add", 10,),
-    ("silu", 8,),
-    ("add", 14,),
-    ("silu", 11,),
-    ("mm8", 17,),
-    ("mm4", 16,),
-    ("mm8", 16,),
-    ("add", 15,),
-    ("store_res", 1, 0, 2, 0, 512,),
-    ("silu", 10,),
-    ("add", 17,),
-    ("silu", 14,),
-    ("store_res", 1, 2, 4, 0, 512,),
+    ("store_res", 0, 2, 4, 0, 512,),
+    ("mm8", 11,),
+    ("mm8", 10,),
+    ("add", 9,),
+    ("silu", 5,),
     ("mm4", 13,),
-    ("add", 16,),
-    ("mm8", 13,),
+    ("quant_w8", 768, 256,),
+    ("silu", 4,),
+    ("quant_w8", 512, 256,),
     ("mm4", 12,),
+    ("silu", 8,),
+    ("store_res", 0, 0, 2, 0, 512,),
+    ("add", 10,),
+    ("cast_res", "G", 0, 384, 128,),
+    ("mm4", 15,),
+    ("silu", 9,),
+    ("mm8", 15,),
+    ("add", 11,),
+    ("cast_res", "G", 0, 128, 128,),
+    ("mm8", 13,),
+    ("silu", 10,),
     ("mm8", 12,),
-    ("silu", 15,),
-    ("cast_res", "V", 1, 256, 256,),
-    ("cast_res", "S", 0, 256, 128,),
-    ("silu", 16,),
-    ("mm4", 18,),
+    ("store_res", 1, 0, 2, 0, 512,),
+    ("add", 15,),
+    ("silu", 11,),
+    ("cast_res", "G", 0, 256, 128,),
+    ("mm4", 14,),
     ("add", 13,),
-    ("mm8", 18,),
+    ("mm8", 14,),
+    ("silu", 15,),
     ("add", 12,),
-    ("silu", 17,),
-    ("mm4", 19,),
-    ("store_res", 0, 2, 4, 512, 512,),
-    ("mm8", 19,),
-    ("quant_res", 0, 0, 256,),
+    ("store_res", 1, 2, 4, 0, 512,),
+    ("mm4", 17,),
     ("silu", 13,),
-    ("add", 18,),
-    ("store_res", 1, 0, 2, 512, 512,),
+    ("mm8", 17,),
+    ("add", 14,),
     ("silu", 12,),
-    ("add", 19,),
-    ("quant_res", 0, 256, 256,),
-    ("silu", 18,),
+    ("mm4", 16,),
+    ("add", 17,),
+    ("mm8", 16,),
+    ("silu", 14,),
+    ("cast_res", "V", 1, 256, 256,),
     ("store_res", 0, 0, 2, 512, 512,),
+    ("mm4", 19,),
+    ("silu", 17,),
+    ("mm8", 19,),
+    ("store_res", 0, 2, 4, 512, 512,),
+    ("add", 16,),
+    ("cast_res", "G", 0, 768, 256,),
+    ("cast_res", "S", 0, 0, 128,),
+    ("mm4", 18,),
+    ("add", 19,),
+    ("mm8", 18,),
+    ("silu", 16,),
+    ("add", 18,),
     ("silu", 19,),
-    ("cast_res", "V", 0, 768, 256,),
-    ("cast_res", "S", 1, 0, 256,),
-    ("cast_res", "S", 1, 768, 256,),
+    ("store_res", 1, 0, 2, 512, 512,),
+    ("quant_res", 0, 0, 256,),
+    ("silu", 18,),
     ("cast_res", "V", 0, 512, 256,),
+    ("cast_res", "S", 1, 0, 256,),
+    ("quant_res", 0, 256, 256,),
     ("store_res", 1, 2, 4, 512, 512,),
     ("quant_res", 0, 768, 256,),
     ("quant_res", 0, 512, 256,),
-    ("cast_res", "V", 1, 512, 256,),
-    ("store_codes", 0, 0, 1024,),
     ("quant_res", 1, 256, 256,),
+    ("cast_res", "S", 1, 768, 256,),
+    ("store_codes", 0, 0, 1024,),
+    ("cast_res", "V", 1, 512, 256,),
     ("quant_res", 1, 0, 256,),
-    ("store_codes", 1, 0, 512,),
     ("quant_res", 1, 512, 256,),
+    ("store_codes", 1, 0, 512,),
     ("quant_res", 1, 768, 256,),
-    ("store_codes", 1, 512, 512,),
-    ("store_scales", "S", 0, 0, 2,),
-    ("store_scales", "SP", 1, 0, 2,),
-    ("store_scales", "SP", 3, 0, 2,),
     ("store_scales", "S", 2, 0, 2,),
+    ("store_scales", "SP", 1, 0, 2,),
+    ("store_scales", "S", 0, 0, 2,),
+    ("store_codes", 1, 512, 512,),
+    ("store_scales", "SP", 3, 0, 2,),
 ]
 
 

from contextlib import ExitStack

import concourse.mybir as mybir
from concourse.masks import make_identity

O, K4, M, T = 512, 1024, 1024, 1024
FLOPS = 2 * (O + K4) * M * T

F32 = mybir.dt.float32
BF16 = mybir.dt.bfloat16
I32 = mybir.dt.int32
U32 = mybir.dt.uint32
U8 = mybir.dt.uint8
FP8X4 = mybir.dt.float8_e4m3fn_x4
FP4X4 = mybir.dt.float4_e2m1fn_x4
SILU = mybir.ActivationFunctionType.Silu
ADD = mybir.AluOpType.add
MULT = mybir.AluOpType.mult

P = 128
PACK = 4
HALF = 512
G4 = 2

UNITS = [("A", 0, 0, 0, 0, 4, 256,), ("A", 0, 1, 0, 1, 4, 256,), ("A", 0, 2, 0, 2, 4, 256,), ("A", 0, 3, 0, 3, 4, 256,), ("A", 0, 0, 256, 4, 4, 256,), ("A", 0, 1, 256, 5, 4, 256,), ("A", 0, 2, 256, 6, 4, 256,), ("A", 0, 3, 256, 7, 4, 256,), ("A", 1, 0, 0, 0, 4, 512,), ("A", 1, 1, 0, 1, 4, 512,), ("A", 1, 2, 0, 2, 4, 512,), ("A", 1, 3, 0, 3, 4, 512,), ("A", 0, 0, 512, 4, 4, 512,), ("A", 0, 1, 512, 5, 4, 512,), ("A", 0, 2, 512, 6, 4, 512,), ("A", 0, 3, 512, 7, 4, 512,), ("A", 1, 0, 512, 0, 4, 512,), ("A", 1, 1, 512, 1, 4, 512,), ("A", 1, 2, 512, 2, 4, 512,), ("A", 1, 3, 512, 3, 4, 512,)]
RES = [(0, 0, 512,), (1, 0, 512,), (0, 512, 512,), (1, 512, 512,)]
DEALT = [0,1]
BB = [5,6,7]
STEPS = [
    ("setup",),
    ("load4", "x4", 0, 1024,),
    ("load_xs", "SP",),
    ("load8", "w8", 0, 256,),
    ("deal_x4", 1, 0,),
    ("load_ws", "SP",),
    ("load4", "w4", 0, 512,),
    ("load8", "x8", 0, 512,),
    ("load8", "w8", 256, 256,),
    ("deal_x4", 0, 0,),
    ("load8", "x8", 512, 512,),
    ("deal_xs", 0,),
    ("load8", "w8", 512, 512,),
    ("load_b", "S",),
    ("cast_w8", "S", 0, 256,),
    ("load4", "w4", 512, 512,),
    ("deal_x4", 0, 1,),
    ("quant_w8", 0, 256,),
    ("mm4", 3,),
    ("deal_x4", 1, 1,),
    ("mm4", 4,),
    ("bcol_tr",),
    ("deal_xs", 1,),
    ("bcol_cp",),
    ("cast_x8", "S", 0, 0,),
    ("bias_tr", 0,),
    ("cast_x8", "V", 0, 1,),
    ("bias_cp", 0,),
    ("bias_tr", 1,),
    ("mm4", 0,),
    ("quant_x8", 0, 1,),
    ("bias_cp", 1,),
    ("mm4", 1,),
    ("mm4", 5,),
    ("cast_w8", "V", 256, 256,),
    ("mm4", 2,),
    ("mm8", 2,),
    ("quant_x8", 0, 0,),
    ("mm4", 6,),
    ("mm8", 3,),
    ("quant_w8", 256, 256,),
    ("mm4", 7,),
    ("add", 2,),
    ("mm8", 1,),
    ("mm8", 0,),
    ("add", 3,),
    ("mm8", 6,),
    ("mm8", 4,),
    ("silu", 2,),
    ("add", 1,),
    ("mm8", 7,),
    ("mm8", 5,),
    ("silu", 3,),
    ("cast_x8", "V", 1, 0,),
    ("cast_x8", "S", 1, 1,),
    ("mm4", 11,),
    ("add", 6,),
    ("mm4", 10,),
    ("add", 0,),
    ("add", 7,),
    ("silu", 6,),
    ("mm4", 9,),
    ("quant_x8", 1, 0,),
    ("silu", 0,),
    ("quant_x8", 1, 1,),
    ("silu", 1,),
    ("mm4", 8,),
    ("add", 4,),
    ("mm8", 8,),
    ("silu", 7,),
    ("add", 5,),
    ("cast_w8", "G", 512, 256,),
    ("mm8", 9,),
    ("cast_w8", "S", 768, 256,),
    ("add", 8,),
    ("store_res", 0, 2, 4, 0, 512,),
    ("mm8", 11,),
    ("mm8", 10,),
    ("add", 9,),
    ("silu", 5,),
    ("mm4", 13,),
    ("quant_w8", 768, 256,),
    ("silu", 4,),
    ("quant_w8", 512, 256,),
    ("mm4", 12,),
    ("silu", 8,),
    ("store_res", 0, 0, 2, 0, 512,),
    ("add", 10,),
    ("cast_res", "G", 0, 384, 128,),
    ("mm4", 15,),
    ("silu", 9,),
    ("mm8", 15,),
    ("add", 11,),
    ("cast_res", "G", 0, 128, 128,),
    ("mm8", 13,),
    ("silu", 10,),
    ("mm8", 12,),
    ("store_res", 1, 0, 2, 0, 512,),
    ("add", 15,),
    ("silu", 11,),
    ("cast_res", "G", 0, 256, 128,),
    ("mm4", 14,),
    ("add", 13,),
    ("mm8", 14,),
    ("silu", 15,),
    ("add", 12,),
    ("store_res", 1, 2, 4, 0, 512,),
    ("mm4", 17,),
    ("silu", 13,),
    ("mm8", 17,),
    ("add", 14,),
    ("silu", 12,),
    ("mm4", 16,),
    ("add", 17,),
    ("mm8", 16,),
    ("silu", 14,),
    ("cast_res", "V", 1, 256, 256,),
    ("store_res", 0, 0, 2, 512, 512,),
    ("mm4", 19,),
    ("silu", 17,),
    ("mm8", 19,),
    ("store_res", 0, 2, 4, 512, 512,),
    ("add", 16,),
    ("cast_res", "G", 0, 768, 256,),
    ("cast_res", "S", 0, 0, 128,),
    ("mm4", 18,),
    ("add", 19,),
    ("mm8", 18,),
    ("silu", 16,),
    ("add", 18,),
    ("silu", 19,),
    ("store_res", 1, 0, 2, 512, 512,),
    ("quant_res", 0, 0, 256,),
    ("silu", 18,),
    ("cast_res", "V", 0, 512, 256,),
    ("cast_res", "S", 1, 0, 256,),
    ("quant_res", 0, 256, 256,),
    ("store_res", 1, 2, 4, 512, 512,),
    ("quant_res", 0, 768, 256,),
    ("quant_res", 0, 512, 256,),
    ("quant_res", 1, 256, 256,),
    ("cast_res", "S", 1, 768, 256,),
    ("store_codes", 0, 0, 1024,),
    ("cast_res", "V", 1, 512, 256,),
    ("quant_res", 1, 0, 256,),
    ("quant_res", 1, 512, 256,),
    ("store_codes", 1, 0, 512,),
    ("quant_res", 1, 768, 256,),
    ("store_scales", "S", 2, 0, 2,),
    ("store_scales", "SP", 1, 0, 2,),
    ("store_scales", "S", 0, 0, 2,),
    ("store_codes", 1, 512, 512,),
    ("store_scales", "SP", 3, 0, 2,),
]


def tile_mix_atom_tm_pl_silu_kernel(
    tc, x8, w8, x4_words, x4_scales, w4_words, w4_scales, b, out_0, out_1, out_2
):
    nc = tc.nc
    with ExitStack() as ctx:
        sb = ctx.enter_context(tc.tile_pool(name="sb", bufs=1))
        ps = ctx.enter_context(tc.psum_pool(name="ps", bufs=1))
        ctx.enter_context(tc.manual_schedule())

        def tile(name, shape, dtype):
            return sb.tile(shape, dtype, name=name, align_bytes=64)

        banks = [ps.tile([P, 512], F32, name="bank%d" % i) for i in range(8)]

        chunks = {"x4": {}, "w4": {}, "x8": {}, "w8": {}}
        xs_raw = tile("xs_raw", [P, G4, T], U8)
        x4_dealt = [[tile("x4_dealt%d_%d" % (a, g), [P, PACK, 2 * P], U8) for g in range(G4)] for a in range(2)]
        xs_dealt = [tile("xs_dealt%d" % a, [P, G4, PACK, P], U8) for a in range(2)]
        ws = tile("ws", [P, G4, M], U8)
        x8_bf = [[tile("x8_bf%d_%d" % (a, s), [P, 2, P, PACK], BF16) for s in range(2)] for a in range(2)]
        x8_codes = [tile("x8_codes%d" % a, [P, PACK * P], U32) for a in range(2)]
        x8_scales = [tile("x8_scales%d" % a, [P, PACK * P], U8) for a in range(2)]
        w8_codes = tile("w8_codes", [P, M], U32)
        w8_scales = tile("w8_scales", [P, M], U8)
        w8_bf = tile("w8_bf", [P, M, PACK], BF16)
        b_rows = tile("b_rows", [P, P], F32)
        b_cols = tile("b_cols", [P, 8], F32)
        ident = tile("ident", [P, P], F32)
        bias = tile("bias", [P, M], F32)
        warm = tile("warm", [P, 8], F32)
        res = {(a, n0): tile("res%d_%d" % (a, n0), [P, PACK, width], F32) for a, n0, width in RES}
        pre = [tile("pre%d" % u, [P, UNITS[u][6]], F32) for u in range(len(UNITS))]
        res_bf = [tile("res_bf%d" % a, [P, M, PACK], BF16) for a in range(2)]
        out_codes = tile("out_codes", [P, 2, M], U32)
        out_scales = tile("out_scales", [P, 2, M], U8)

        def cast(eng, dst, src):
            if eng == "V":
                nc.vector.tensor_copy(out=dst, in_=src)
            elif eng == "S":
                nc.scalar.copy(out=dst, in_=src)
            else:
                nc.gpsimd.tensor_scalar(out=dst, in0=src, scalar1=1.0, scalar2=-0.0, op0=MULT, op1=ADD)

        def interleave(eng, dst, src):
            cast(eng, dst.rearrange("p (c i) j -> p c j i", i=4), src.rearrange("p j (c i) -> p c j i", i=4))

        def cols(kind, c0, width, per=1):
            first = max(c for c in chunks[kind] if c <= c0)
            return chunks[kind][first][:, :, per * (c0 - first) : per * (c0 - first + width)]

        def res_cols(a, c0, width):
            first = max(n0 for aa, n0 in res if aa == a and n0 <= c0)
            return res[(a, first)][:, :, c0 - first : c0 - first + width]

        def load_scales(queue, plane, scales):
            for r in range(4):
                queue.dma_start(
                    out=plane[r:P:32, :, :].bitcast(I32),
                    in_=scales.rearrange("g (q r) n -> r q g n", r=4)[r].bitcast(I32),
                )

        def load4(kind, c0, width):
            words = x4_words if kind == "x4" else w4_words
            raw = tile("%s_raw%d" % (kind, c0), [P, G4, 2 * width], U8)
            chunks[kind][c0] = raw
            nc.sync.dma_start(
                out=raw[:].bitcast(I32),
                in_=words[:, :, 2 * c0 : 2 * (c0 + width)].rearrange("g p c -> p g c").bitcast(I32),
            )

        def load8(kind, c0, width):
            src = x8 if kind == "x8" else w8
            raw = tile("%s_raw%d" % (kind, c0), [P, PACK, width], F32)
            chunks[kind][c0] = raw
            nc.sync.dma_start(out=raw[:], in_=src[:, c0 : c0 + width].rearrange("(p j) n -> p j n", j=PACK))

        def bcol_tr():
            nc.tensor.transpose(banks[BB[0]][:, 0:P], b_rows[:], ident[:])

        def bcol_cp():
            nc.scalar.copy(out=b_cols[:], in_=banks[BB[0]][:, 0:8])

        def bias_tr(half):
            for e in range(4):
                c = 4 * half + e
                nc.tensor.transpose(
                    banks[BB[1 + half]][:, P * e : P * (e + 1)], b_cols[:, c : c + 1].to_broadcast([P, P]), ident[:]
                )

        def bias_cp(half):
            nc.scalar.copy(out=bias[:, HALF * half : HALF * (half + 1)], in_=banks[BB[1 + half]][:])

        def deal_x4(a, g):
            nc.vector.tensor_copy(
                out=x4_dealt[a][g][:].rearrange("p r (m y) -> p r m y", y=2),
                in_=cols("x4", HALF * a, HALF, 2)[:, g, :].rearrange("p (m r y) -> p r m y", r=PACK, y=2),
            )

        def deal_xs(a):
            nc.vector.tensor_copy(
                out=xs_dealt[a][:],
                in_=xs_raw[:, :, HALF * a : HALF * (a + 1)].rearrange("p g (m r) -> p g r m", r=PACK),
            )

        def cast_x8(eng, a, s):
            if a in DEALT:
                cast(
                    eng,
                    x8_bf[a][s][:].rearrange("p r m j -> p m j r"),
                    cols("x8", HALF * a, HALF).rearrange("p j (m r) -> p m j r", r=PACK)[:, :, :, 2 * s : 2 * s + 2],
                )
            else:
                interleave(eng, x8_bf[a][s][:].rearrange("p r m j -> p (r m) j"), cols("x8", HALF * a + 256 * s, 256))

        def quant_x8(a, s):
            span = slice(2 * P * s, 2 * P * (s + 1))
            nc.vector.quantize_mx(
                out=x8_codes[a][:, span].bitcast(FP8X4),
                scales=x8_scales[a][:, span],
                in_=x8_bf[a][s][:].rearrange("p r m j -> p (r m j)"),
            )

        def cast_w8(eng, n0, width):
            interleave(eng, w8_bf[:, n0 : n0 + width, :], cols("w8", n0, width))

        def quant_w8(n0, width):
            nc.vector.quantize_mx(
                out=w8_codes[:, n0 : n0 + width].bitcast(FP8X4),
                scales=w8_scales[:, n0 : n0 + width],
                in_=w8_bf[:, n0 : n0 + width, :].rearrange("p c j -> p (c j)"),
            )

        def mm4(u):
            kind, a, i, n0, bank, first, width = UNITS[u]
            for g in range(G4):
                if kind == "A":
                    x, xs = x4_dealt[a][g][:, i, :], xs_dealt[a][:, g, i, :]
                    w, wsc = cols("w4", n0, width, 2)[:, g, :], ws[:, g, n0 : n0 + width]
                    ops = (x, xs, w, wsc)
                else:
                    x, xs = cols("x4", HALF * a, HALF, 2)[:, g, :], xs_raw[:, g, HALF * a : HALF * (a + 1)]
                    w, wsc = cols("w4", n0, P, 2)[:, g, :], ws[:, g, n0 : n0 + P]
                    ops = (w, wsc, x, xs)
                nc.tensor.matmul_mx(
                    out=banks[bank][:, 0:width],
                    lhsT=ops[0].bitcast(FP4X4),
                    lhsT_scale=ops[1],
                    rhs=ops[2].bitcast(FP4X4),
                    rhs_scale=ops[3],
                    start=(g == 0 and first == 4),
                    stop=(g == G4 - 1 and first == 8),
                )

        def mm8(u):
            kind, a, i, n0, bank, first, width = UNITS[u]
            if kind == "A":
                ops = (x8_codes[a][:, P * i : P * (i + 1)], x8_scales[a][:, P * i : P * (i + 1)],
                       w8_codes[:, n0 : n0 + width], w8_scales[:, n0 : n0 + width])
            else:
                ops = (w8_codes[:, n0 : n0 + P], w8_scales[:, n0 : n0 + P], x8_codes[a][:], x8_scales[a][:])
            nc.tensor.matmul_mx(
                out=banks[bank][:, 0:width],
                lhsT=ops[0].bitcast(FP8X4),
                lhsT_scale=ops[1],
                rhs=ops[2].bitcast(FP8X4),
                rhs_scale=ops[3],
                start=(first == 8),
                stop=(first == 4),
            )

        def add_bias(u):
            kind, a, i, n0, bank, first, width = UNITS[u]
            nc.vector.tensor_tensor(out=pre[u][:], in0=banks[bank][:, 0:width], in1=bias[:, n0 : n0 + width], op=ADD)

        def silu(u):
            kind, a, i, n0, bank, first, width = UNITS[u]
            if kind == "A":
                nc.scalar.activation(out=res_cols(a, n0, width)[:, i, :], in_=pre[u][:], func=SILU)
            else:
                nc.scalar.activation(
                    out=pre[u][:].rearrange("p (r m) -> p r m", r=PACK),
                    in_=banks[bank][:].rearrange("p (m r) -> p r m", r=PACK),
                    func=SILU,
                    bias=b_cols[:, n0 // P : n0 // P + 1],
                )

        def turn(u):
            kind, a, i, n0, bank, first, width = UNITS[u]
            for r in range(PACK):
                nc.tensor.transpose(banks[i][:, P * r : P * (r + 1)], pre[u][:, P * r : P * (r + 1)], ident[:])

        def cast_out(eng, u):
            kind, a, i, n0, bank, first, width = UNITS[u]
            cast(eng, res_cols(a, n0, P), banks[i][:].rearrange("p (r n) -> p r n", r=PACK))

        def cast_res(eng, a, c0, width):
            interleave(eng, res_bf[a][:, c0 : c0 + width, :], res_cols(a, c0, width))

        def quant_res(a, c0, width):
            nc.vector.quantize_mx(
                out=out_codes[:, a, c0 : c0 + width].bitcast(FP8X4),
                scales=out_scales[:, a, c0 : c0 + width],
                in_=res_bf[a][:, c0 : c0 + width, :].rearrange("p c j -> p (c j)"),
            )

        def store_res(a, r0, r1, n0, width):
            nc.sync.dma_start(
                out=out_0[HALF * a : HALF * (a + 1), n0 : n0 + width].rearrange("(p r) n -> p r n", r=PACK)[:, r0:r1, :],
                in_=res_cols(a, n0, width)[:, r0:r1, :],
            )

        def store_codes(a, n0, width):
            nc.sync.dma_start(
                out=out_1[a].rearrange("p n i -> p (n i)").bitcast(I32)[:, n0 : n0 + width],
                in_=out_codes[:, a, n0 : n0 + width].bitcast(I32),
            )

        def store_scales(queue, r, a0, a1):
            queue.dma_start(
                out=out_2.rearrange("g (q r) n -> r q g n", r=4)[r][:, a0:a1, :].bitcast(I32),
                in_=out_scales[r:P:32, a0:a1, :].bitcast(I32),
            )

        def setup():
            nc.vector.memset(xs_raw[:].rearrange("p g t -> p (g t)").bitcast(I32), 0)
            nc.vector.memset(warm[:, 1:2], 0.0)
            nc.vector.memset(b_rows[:], 0.0)
            nc.vector.memset(ident[:], 0.0)
            nc.vector.memset(ws[:].rearrange("p g t -> p (g t)").bitcast(I32), 0)
            make_identity(nc, ident[:], nomemset=True)
            nc.scalar.activation(out=warm[:, 0:1], in_=warm[:, 1:2], func=SILU)

        def load_b(e):
            queues[e].dma_start(out=b_rows[0:8, :], in_=b.rearrange("(c p) -> c p", p=P))

        queues = {"SP": nc.sync, "S": nc.scalar}
        table = {
            "setup": setup,
            "load_b": load_b,
            "load_xs": lambda e: load_scales(queues[e], xs_raw, x4_scales),
            "load_ws": lambda e: load_scales(queues[e], ws, w4_scales),
            "load4": load4,
            "load8": load8,
            "bias_tr": bias_tr,
            "bcol_tr": bcol_tr,
            "bcol_cp": bcol_cp,
            "turn": turn,
            "cast_out": cast_out,
            "bias_cp": bias_cp,
            "deal_x4": deal_x4,
            "deal_xs": deal_xs,
            "cast_x8": cast_x8,
            "quant_x8": quant_x8,
            "cast_w8": cast_w8,
            "quant_w8": quant_w8,
            "mm4": mm4,
            "mm8": mm8,
            "add": add_bias,
            "silu": silu,
            "cast_res": cast_res,
            "quant_res": quant_res,
            "store_res": store_res,
            "store_codes": store_codes,
            "store_scales": lambda e, r, a0, a1: store_scales(queues[e], r, a0, a1),
        }
        for step in STEPS:
            table[step[0]](*step[1:])
